import numpy as np
import ml_dtypes


def mxq(x, axis, fmt="e4m3"):
    dtype, down = {"e4m3": (ml_dtypes.float8_e4m3fn, 7), "e5m2": (ml_dtypes.float8_e5m2, 14)}[fmt]
    v = np.moveaxis(np.asarray(x, np.float32).astype(ml_dtypes.bfloat16).astype(np.float64), axis, -1)
    blocks = v.reshape(v.shape[:-1] + (-1, 32))
    amax = np.abs(blocks).max(-1, keepdims=True)
    byte = np.maximum(np.where(amax > 0, np.frexp(amax)[1] - 1 + 127, 0) - down, 1)
    scale = np.exp2(byte - 127.0)
    codes = (blocks / scale).astype(np.float32).astype(dtype).astype(np.float64)
    return np.moveaxis((codes * scale).reshape(v.shape), -1, axis)


WIDE = False


def mx_kscale(k):
    if not WIDE:
        return np.ones(k)
    levels = np.array([10, -10, 5, -5, 0])
    if k % 512:
        return np.exp2(np.random.permutation(np.resize(levels, k // 32))).repeat(32)
    a = np.empty((k // 512, 16))
    for p in range(k // 512):
        a[p, :8] = np.random.permutation(np.resize(levels, 8))
        for g in range(8):
            far = levels[np.abs(levels - a[p, g]) >= 10]
            a[p, g + 8] = far[np.random.randint(len(far))]
    return np.exp2(a.ravel()).repeat(32)


def f64(x):
    return np.asarray(x).astype(np.float64)


def striped(idx):
    return np.tile(idx.reshape(-1, 16).T, (8, 1)).astype(np.uint16)


def unstriped(offs):
    return offs[:16].T.reshape(-1).astype(np.int64)


def striped8(idx):
    return np.concatenate([x.reshape(-1, 16).T for x in idx]).astype(np.uint16)


def runs(offs, k):
    lists = np.stack([offs[16 * r : 16 * r + 16].T.reshape(-1) for r in range(8)]).astype(np.int64)
    return lists[np.arange(k) % 512 // 64]


def pack_weight(w):
    k, n = w.shape
    w = f64(np.asarray(w, np.float32).astype(ml_dtypes.bfloat16)).reshape(k // 32, 32, n)
    amax = np.abs(w).max(1)
    byte = np.clip(np.where(amax > 0, np.frexp(amax)[1] - 1 + 127 - 7, 1), 1, 254)
    scaled = (w * np.exp2(127.0 - byte)[:, None, :]).reshape(k, n).astype(np.float32)
    words = np.ascontiguousarray(scaled.reshape(k // 512, 128, 4, n).transpose(0, 1, 3, 2)).astype(ml_dtypes.float8_e4m3fn).view(np.uint8)
    return words, np.ascontiguousarray(byte.astype(np.uint8).reshape(k // 512, 16, n))


def unpack_weight(words, scales):
    g, p, n, _ = words.shape
    vals = np.ascontiguousarray(words).view(ml_dtypes.float8_e4m3fn).astype(np.float64) * np.repeat(np.exp2(scales.astype(np.float64) - 127.0), 8, axis=1)[..., None]
    return vals.transpose(0, 1, 3, 2).reshape(g * 512, n)


def relu(v):
    return np.maximum(v, 0.0)


def sigmoid(v):
    return 1.0 / (1.0 + np.exp(-np.maximum(v, -700.0)))


K, T, S, N, H = 512, 2048, 512, 512, 512


def setup_inputs():
    n = np.random.standard_normal
    s = mx_kscale(K)[:, None]
    u = mx_kscale(H)
    packed_xT = pack_weight(n((K, T)) * s)
    return {
        "x_words": packed_xT[0],
        "x_scales": packed_xT[1],
        "w1": (n((K, H)) / np.sqrt(K) / s * u).astype(np.float32),
        "w2": (n((K, H)) / np.sqrt(K) / s).astype(np.float32),
        "w3": (n((H, N)) / np.sqrt(H) / u[:, None]).astype(np.float32),
        "offs": striped(np.random.permutation(T)[:S]),
        "mix": striped(np.random.permutation(T)[:S]),
        "al": striped8(np.stack([np.random.permutation(S) for _ in range(8)])),
    }


def reference(x_words, x_scales, w1, w2, w3, offs, mix, al):
    x_mix = unpack_weight(x_words, x_scales)[:, unstriped(mix)]
    e = relu(mxq(f64(w1), 0, "e4m3").T @ x_mix)
    xq = unpack_weight(x_words, x_scales)[:, unstriped(offs)]
    s = mxq(f64(w2), 0, "e4m3").T @ xq
    mk = sigmoid(s)
    z = e * (mk[np.arange(H)[:, None], runs(al, H)])
    return mxq(f64(w3), 0, "e4m3").T @ mxq(z, 0, "e4m3")

@@ -1,0 +1,148 @@
+from contextlib import ExitStack
+
+import concourse.mybir as mybir
+
+K, T, S, H, N = 512, 2048, 512, 512, 512
+FLOPS = 2 * K * H * S * 2 + 2 * H * N * S
+
+F32 = mybir.dt.float32
+BF16 = mybir.dt.bfloat16
+I32 = mybir.dt.int32
+U32 = mybir.dt.uint32
+U16 = mybir.dt.uint16
+U8 = mybir.dt.uint8
+FP8X4 = mybir.dt.float8_e4m3fn_x4
+ALU = mybir.AluOpType
+ACT = mybir.ActivationFunctionType
+
+P = 128
+PACK = 4
+HALF = 256
+CHUNK = 128
+GATHERS = [(0, 256), (256, 128), (384, 128)]
+
+
+def tile_picked_maskdec_relu_p_kernel(tc, x_words, x_scales, w1, w2, w3, offs, mix, al, out):
+    nc = tc.nc
+    with ExitStack() as ctx:
+        keep = ctx.enter_context(tc.tile_pool(name="keep", bufs=1))
+        psum = ctx.enter_context(tc.psum_pool(name="psum", bufs=1))
+
+        def sb(name, shape, dtype):
+            return keep.tile(shape, dtype, name=name, align_bytes=64)
+
+        offs_sb = sb("offs_sb", [P, S // 16], U16)
+        mix_sb = sb("mix_sb", [P, S // 16], U16)
+        al_sb = sb("al_sb", [P, S // 16], U16)
+        xw = sb("xw", [P, T], I32)
+        xs = sb("xs", [P, T], U8)
+        warm = sb("warm", [P, 8], F32)
+        warm2 = sb("warm2", [P, 8], F32)
+
+        nc.vector.memset(xs[:].bitcast(I32), 0)
+        nc.vector.memset(warm[:], 0.0)
+        nc.scalar.activation(warm2[:], warm[:], ACT.Sigmoid)
+
+        nc.sync.dma_start(out=xw[:], in_=x_words[0].rearrange("p c r -> p (c r)").bitcast(I32))
+        nc.sync.dma_start(offs_sb[:], offs)
+        for q in range(4):
+            nc.sync.dma_start(out=xs[32 * q : 32 * q + 4, :].bitcast(I32), in_=x_scales[0, 4 * q : 4 * q + 4, :].bitcast(I32))
+
+        def load_w(name, w, between_sb=None, between=None):
+            halves = []
+            for h in range(2):
+                raw = sb(name + "_raw%d" % h, [P, PACK, HALF], F32)
+                nc.sync.dma_start(out=raw[:], in_=w[:, h * HALF : (h + 1) * HALF].rearrange("(p j) c -> p j c", j=PACK))
+                halves.append(raw)
+                if h == 0 and between_sb is not None:
+                    nc.sync.dma_start(between_sb[:], between)
+            return halves
+
+        w2_raw = load_w("w2", w2)
+        w1_raw = load_w("w1", w1, mix_sb, mix)
+        nc.sync.dma_start(al_sb[:], al)
+        w3_raw = load_w("w3", w3)
+
+        def cast(engine, dst, src):
+            if engine == "s":
+                nc.scalar.copy(out=dst, in_=src)
+            else:
+                nc.vector.tensor_copy(out=dst, in_=src)
+
+        def cast_dealt(engine, grouped, raw, h):
+            dst = grouped[:].rearrange("p (t m j) -> p m j t", t=PACK, j=PACK)[:, 64 * h : 64 * (h + 1)]
+            cast(engine, dst, raw[:].rearrange("p j (m t) -> p m j t", t=PACK))
+
+        def cast_plain(engine, grouped, raw, h):
+            dst = grouped[:].rearrange("p (m i j) -> p m j i", i=PACK, j=PACK)[:, 64 * h : 64 * (h + 1)]
+            cast(engine, dst, raw[:].rearrange("p j (m i) -> p m j i", i=PACK))
+
+        def quantize(codes, scales, grouped, c0, c1):
+            nc.vector.quantize_mx(out=codes[:, c0:c1].bitcast(FP8X4), scales=scales[:, c0:c1], in_=grouped[:, PACK * c0 : PACK * c1])
+
+        def pick(name, lst):
+            words = sb(name + "_words", [P, S], U32)
+            scales = sb(name + "_scales", [P, S], U8)
+            nc.vector.tensor_copy(out=words[:], in_=xw[:].bitcast(U32).indirect(lst[:]))
+            nc.vector.tensor_copy(out=scales[:], in_=xs[:].indirect(lst[:]))
+            return words, scales
+
+        def mx(dst, wc, ws, m, xc, xsc, cols):
+            nc.tensor.matmul_mx(out=dst, lhsT=wc[:, m * P : (m + 1) * P].bitcast(FP8X4), lhsT_scale=ws[:, m * P : (m + 1) * P],
+                                rhs=xc[:, cols].bitcast(FP8X4), rhs_scale=xsc[:, cols], start=True, stop=True)
+
+        w_bf = [sb("w%d_bf" % i, [P, PACK * H], BF16) for i in (1, 2, 3)]
+        w_codes = [sb("w%d_codes" % i, [P, H], U32) for i in (1, 2, 3)]
+        w_scales = [sb("w%d_scales" % i, [P, H], U8) for i in (1, 2, 3)]
+
+        q_words, q_scales = pick("q", offs_sb)
+        cast_dealt("s", w_bf[1], w2_raw[0], 0)
+        cast_dealt("v", w_bf[1], w2_raw[1], 1)
+        for t in range(PACK):
+            quantize(w_codes[1], w_scales[1], w_bf[1], t * P, (t + 1) * P)
+        s_sb = []
+        for t in range(PACK):
+            bank = psum.tile([P, S], F32, name="s_bank%d" % t, tag="a%d" % t)
+            mx(bank[:], w_codes[1], w_scales[1], t, q_words, q_scales, slice(0, S))
+            s_t = sb("s_sb%d" % t, [P, S], F32)
+            nc.scalar.copy(out=s_t[:], in_=bank[:])
+            s_sb.append(s_t)
+
+        m_words, m_scales = pick("m", mix_sb)
+        cast_dealt("v", w_bf[0], w1_raw[0], 0)
+        cast_dealt("v", w_bf[0], w1_raw[1], 1)
+        quantize(w_codes[0], w_scales[0], w_bf[0], 0, H)
+        e_banks = []
+        for c in range(S // CHUNK):
+            bank = psum.tile([P, PACK, CHUNK], F32, name="e_bank%d" % c, tag="e%d" % c)
+            for t in range(PACK):
+                mx(bank[:, t, :], w_codes[0], w_scales[0], t, m_words, m_scales, slice(c * CHUNK, (c + 1) * CHUNK))
+            e_banks.append(bank)
+
+        cast_plain("v", w_bf[2], w3_raw[0], 0)
+        cast_plain("v", w_bf[2], w3_raw[1], 1)
+        quantize(w_codes[2], w_scales[2], w_bf[2], 0, N)
+
+        out_rows = out.rearrange("(m p) j -> p m j", p=P)
+        for j0, width in GATHERS:
+            mask = sb("mask%d" % j0, [P, PACK, width], F32)
+            for t in range(PACK):
+                nc.scalar.activation(mask[:, t, :], s_sb[t][:].indirect(al_sb[:, j0 // 16 : (j0 + width) // 16]), ACT.Sigmoid)
+            for c in range(j0 // CHUNK, (j0 + width) // CHUNK):
+                lo = c * CHUNK - j0
+                z_bf = sb("z_bf%d" % c, [P, CHUNK * PACK], BF16)
+                nc.vector.scalar_tensor_tensor(
+                    out=z_bf[:].rearrange("p (n t) -> p n t", t=PACK),
+                    in0=e_banks[c][:].rearrange("p t n -> p n t"),
+                    scalar=0.0,
+                    in1=mask[:, :, lo : lo + CHUNK].rearrange("p t n -> p n t"),
+                    op0=ALU.max, op1=ALU.mult)
+                z_codes = sb("z_codes%d" % c, [P, CHUNK], U32)
+                z_scales = sb("z_scales%d" % c, [P, CHUNK], U8)
+                quantize(z_codes, z_scales, z_bf, 0, CHUNK)
+                bank = psum.tile([P, PACK, CHUNK], F32, name="o_bank%d" % c, tag="a%d" % c)
+                for m in range(N // P):
+                    mx(bank[:, m, :], w_codes[2], w_scales[2], m, z_codes, z_scales, slice(0, CHUNK))
+                res = sb("res%d" % c, [P, PACK, CHUNK], F32)
+                cast("s" if c < 3 else "v", res[:], bank[:])
+                nc.sync.dma_start(out=out_rows[:, :, c * CHUNK : (c + 1) * CHUNK], in_=res[:])

@@ -17,9 +17,9 @@ ACT = mybir.ActivationFunctionType
 
 P = 128
 PACK = 4
-HALF = 256
 CHUNK = 128
-GATHERS = [(0, 256), (256, 128), (384, 128)]
+W2_SPLIT = 256
+STRETCHES = [(0, 256), (256, 128), (384, 128)]
 
 
 def tile_picked_maskdec_relu_p_kernel(tc, x_words, x_scales, w1, w2, w3, offs, mix, al, out):
@@ -28,121 +28,123 @@ def tile_picked_maskdec_relu_p_kernel(tc, x_words, x_scales, w1, w2, w3, offs, m
         keep = ctx.enter_context(tc.tile_pool(name="keep", bufs=1))
         psum = ctx.enter_context(tc.psum_pool(name="psum", bufs=1))
 
-        def sb(name, shape, dtype):
-            return keep.tile(shape, dtype, name=name, align_bytes=64)
+        def sb(name, shape, dtype, tag=None):
+            return keep.tile(shape, dtype, name=name, tag=tag or name, align_bytes=64)
 
         offs_sb = sb("offs_sb", [P, S // 16], U16)
         mix_sb = sb("mix_sb", [P, S // 16], U16)
         al_sb = sb("al_sb", [P, S // 16], U16)
         xw = sb("xw", [P, T], I32)
         xs = sb("xs", [P, T], U8)
-        warm = sb("warm", [P, 8], F32)
-        warm2 = sb("warm2", [P, 8], F32)
+        warm_in = sb("warm_in", [P, 8], F32)
+        warm_out = sb("warm_out", [P, 8], F32)
 
         nc.vector.memset(xs[:].bitcast(I32), 0)
-        nc.vector.memset(warm[:], 0.0)
-        nc.scalar.activation(warm2[:], warm[:], ACT.Sigmoid)
+        nc.vector.memset(warm_in[:], 0.0)
+        nc.scalar.activation(warm_out[:], warm_in[:], ACT.Sigmoid)
+
+        def load_rows(name, w, c0, c1):
+            raw = sb(name, [P, PACK, c1 - c0], F32)
+            nc.sync.dma_start(out=raw[:], in_=w[:, c0:c1].rearrange("(p j) c -> p j c", j=PACK))
+            return raw
 
         nc.sync.dma_start(out=xw[:], in_=x_words[0].rearrange("p c r -> p (c r)").bitcast(I32))
         nc.sync.dma_start(offs_sb[:], offs)
         for q in range(4):
             nc.sync.dma_start(out=xs[32 * q : 32 * q + 4, :].bitcast(I32), in_=x_scales[0, 4 * q : 4 * q + 4, :].bitcast(I32))
-
-        def load_w(name, w, between_sb=None, between=None):
-            halves = []
-            for h in range(2):
-                raw = sb(name + "_raw%d" % h, [P, PACK, HALF], F32)
-                nc.sync.dma_start(out=raw[:], in_=w[:, h * HALF : (h + 1) * HALF].rearrange("(p j) c -> p j c", j=PACK))
-                halves.append(raw)
-                if h == 0 and between_sb is not None:
-                    nc.sync.dma_start(between_sb[:], between)
-            return halves
-
-        w2_raw = load_w("w2", w2)
-        w1_raw = load_w("w1", w1, mix_sb, mix)
+        nc.sync.dma_start(mix_sb[:], mix)
+        w2_left = load_rows("w2_left", w2, 0, W2_SPLIT)
+        w2_right = load_rows("w2_right", w2, W2_SPLIT, H)
         nc.sync.dma_start(al_sb[:], al)
-        w3_raw = load_w("w3", w3)
+        w1_raw = load_rows("w1_raw", w1, 0, H)
+        w3_raw = load_rows("w3_raw", w3, 0, N)
 
-        def cast(engine, dst, src):
-            if engine == "s":
-                nc.scalar.copy(out=dst, in_=src)
-            else:
-                nc.vector.tensor_copy(out=dst, in_=src)
+        def dealt(grouped):
+            return grouped[:].rearrange("p (t m j) -> p m j t", t=PACK, j=PACK)
 
-        def cast_dealt(engine, grouped, raw, h):
-            dst = grouped[:].rearrange("p (t m j) -> p m j t", t=PACK, j=PACK)[:, 64 * h : 64 * (h + 1)]
-            cast(engine, dst, raw[:].rearrange("p j (m t) -> p m j t", t=PACK))
+        def by_four(raw):
+            return raw[:].rearrange("p j (m t) -> p m j t", t=PACK)
 
-        def cast_plain(engine, grouped, raw, h):
-            dst = grouped[:].rearrange("p (m i j) -> p m j i", i=PACK, j=PACK)[:, 64 * h : 64 * (h + 1)]
-            cast(engine, dst, raw[:].rearrange("p j (m i) -> p m j i", i=PACK))
+        def quantize(name, grouped, width, pieces):
+            codes = sb(name + "_codes", [P, width], U32)
+            scales = sb(name + "_scales", [P, width], U8)
+            step = width // pieces
+            for c0 in range(0, width, step):
+                nc.vector.quantize_mx(out=codes[:, c0 : c0 + step].bitcast(FP8X4), scales=scales[:, c0 : c0 + step], in_=grouped[:, PACK * c0 : PACK * (c0 + step)])
+            return codes, scales
 
-        def quantize(codes, scales, grouped, c0, c1):
-            nc.vector.quantize_mx(out=codes[:, c0:c1].bitcast(FP8X4), scales=scales[:, c0:c1], in_=grouped[:, PACK * c0 : PACK * c1])
+        def product(dst, weights, m, moving, cols):
+            nc.tensor.matmul_mx(
+                out=dst,
+                lhsT=weights[0][:, m * P : (m + 1) * P].bitcast(FP8X4),
+                lhsT_scale=weights[1][:, m * P : (m + 1) * P],
+                rhs=moving[0][:, cols].bitcast(FP8X4),
+                rhs_scale=moving[1][:, cols],
+                start=True,
+                stop=True,
+            )
 
-        def pick(name, lst):
-            words = sb(name + "_words", [P, S], U32)
-            scales = sb(name + "_scales", [P, S], U8)
-            nc.vector.tensor_copy(out=words[:], in_=xw[:].bitcast(U32).indirect(lst[:]))
-            nc.vector.tensor_copy(out=scales[:], in_=xs[:].indirect(lst[:]))
-            return words, scales
+        q_words = sb("q_words", [P, S], U32)
+        q_scales = sb("q_scales", [P, S], U8)
+        m_words = sb("m_words", [P, S], U32)
+        nc.vector.tensor_copy(out=q_words[:], in_=xw[:].bitcast(U32).indirect(offs_sb[:]))
+        nc.vector.tensor_copy(out=q_scales[:], in_=xs[:].indirect(offs_sb[:]))
+        nc.vector.tensor_copy(out=m_words[:], in_=xw[:].bitcast(U32).indirect(mix_sb[:]))
 
-        def mx(dst, wc, ws, m, xc, xsc, cols):
-            nc.tensor.matmul_mx(out=dst, lhsT=wc[:, m * P : (m + 1) * P].bitcast(FP8X4), lhsT_scale=ws[:, m * P : (m + 1) * P],
-                                rhs=xc[:, cols].bitcast(FP8X4), rhs_scale=xsc[:, cols], start=True, stop=True)
-
-        w_bf = [sb("w%d_bf" % i, [P, PACK * H], BF16) for i in (1, 2, 3)]
-        w_codes = [sb("w%d_codes" % i, [P, H], U32) for i in (1, 2, 3)]
-        w_scales = [sb("w%d_scales" % i, [P, H], U8) for i in (1, 2, 3)]
-
-        q_words, q_scales = pick("q", offs_sb)
-        cast_dealt("s", w_bf[1], w2_raw[0], 0)
-        cast_dealt("v", w_bf[1], w2_raw[1], 1)
-        for t in range(PACK):
-            quantize(w_codes[1], w_scales[1], w_bf[1], t * P, (t + 1) * P)
+        w2_bf = sb("w2_bf", [P, PACK * H], BF16)
+        nc.scalar.copy(out=dealt(w2_bf)[:, : W2_SPLIT // PACK], in_=by_four(w2_left))
+        nc.vector.tensor_copy(out=dealt(w2_bf)[:, W2_SPLIT // PACK :], in_=by_four(w2_right))
+        w2_mx = quantize("w2", w2_bf, H, 2)
         s_sb = []
         for t in range(PACK):
             bank = psum.tile([P, S], F32, name="s_bank%d" % t, tag="a%d" % t)
-            mx(bank[:], w_codes[1], w_scales[1], t, q_words, q_scales, slice(0, S))
+            product(bank[:], w2_mx, t, (q_words, q_scales), slice(0, S))
             s_t = sb("s_sb%d" % t, [P, S], F32)
             nc.scalar.copy(out=s_t[:], in_=bank[:])
             s_sb.append(s_t)
 
-        m_words, m_scales = pick("m", mix_sb)
-        cast_dealt("v", w_bf[0], w1_raw[0], 0)
-        cast_dealt("v", w_bf[0], w1_raw[1], 1)
-        quantize(w_codes[0], w_scales[0], w_bf[0], 0, H)
+        m_scales = sb("m_scales", [P, S], U8, tag="w2_bf")
+        nc.vector.tensor_copy(out=m_scales[:], in_=xs[:].indirect(mix_sb[:]))
+        w1_bf = sb("w1_bf", [P, PACK * H], BF16)
+        nc.vector.tensor_copy(out=dealt(w1_bf), in_=by_four(w1_raw))
+        w1_mx = quantize("w1", w1_bf, H, 1)
         e_banks = []
         for c in range(S // CHUNK):
             bank = psum.tile([P, PACK, CHUNK], F32, name="e_bank%d" % c, tag="e%d" % c)
             for t in range(PACK):
-                mx(bank[:, t, :], w_codes[0], w_scales[0], t, m_words, m_scales, slice(c * CHUNK, (c + 1) * CHUNK))
+                product(bank[:, t, :], w1_mx, t, (m_words, m_scales), slice(c * CHUNK, (c + 1) * CHUNK))
             e_banks.append(bank)
 
-        cast_plain("v", w_bf[2], w3_raw[0], 0)
-        cast_plain("v", w_bf[2], w3_raw[1], 1)
-        quantize(w_codes[2], w_scales[2], w_bf[2], 0, N)
+        w3_bf = sb("w3_bf", [P, PACK * N], BF16)
+        nc.vector.tensor_copy(out=w3_bf[:].rearrange("p (m i j) -> p m j i", i=PACK, j=PACK), in_=by_four(w3_raw))
+        w3_mx = quantize("w3", w3_bf, N, 1)
 
         out_rows = out.rearrange("(m p) j -> p m j", p=P)
-        for j0, width in GATHERS:
+        free_banks = ["a0", "a1", "a2", "a3", "e0"]
+        for j0, width in STRETCHES:
             mask = sb("mask%d" % j0, [P, PACK, width], F32)
             for t in range(PACK):
                 nc.scalar.activation(mask[:, t, :], s_sb[t][:].indirect(al_sb[:, j0 // 16 : (j0 + width) // 16]), ACT.Sigmoid)
-            for c in range(j0 // CHUNK, (j0 + width) // CHUNK):
-                lo = c * CHUNK - j0
-                z_bf = sb("z_bf%d" % c, [P, CHUNK * PACK], BF16)
+            z_bf = sb("z_bf%d" % j0, [P, width * PACK], BF16, tag="w3_bf")
+            for lo in range(0, width, CHUNK):
                 nc.vector.scalar_tensor_tensor(
-                    out=z_bf[:].rearrange("p (n t) -> p n t", t=PACK),
-                    in0=e_banks[c][:].rearrange("p t n -> p n t"),
+                    out=z_bf[:, lo * PACK : (lo + CHUNK) * PACK].rearrange("p (n t) -> p n t", t=PACK),
+                    in0=e_banks[(j0 + lo) // CHUNK][:].rearrange("p t n -> p n t"),
                     scalar=0.0,
                     in1=mask[:, :, lo : lo + CHUNK].rearrange("p t n -> p n t"),
-                    op0=ALU.max, op1=ALU.mult)
-                z_codes = sb("z_codes%d" % c, [P, CHUNK], U32)
-                z_scales = sb("z_scales%d" % c, [P, CHUNK], U8)
-                quantize(z_codes, z_scales, z_bf, 0, CHUNK)
-                bank = psum.tile([P, PACK, CHUNK], F32, name="o_bank%d" % c, tag="a%d" % c)
-                for m in range(N // P):
-                    mx(bank[:, m, :], w_codes[2], w_scales[2], m, z_codes, z_scales, slice(0, CHUNK))
-                res = sb("res%d" % c, [P, PACK, CHUNK], F32)
-                cast("s" if c < 3 else "v", res[:], bank[:])
-                nc.sync.dma_start(out=out_rows[:, :, c * CHUNK : (c + 1) * CHUNK], in_=res[:])
+                    op0=ALU.max,
+                    op1=ALU.mult,
+                )
+            z_mx = quantize("z%d" % j0, z_bf, width, 1)
+            last = j0 + width == S
+            per_bank = 2 if last else S // width
+            for m0 in range(0, N // P, per_bank):
+                bank = psum.tile([P, per_bank, width], F32, name="o_bank%d_%d" % (j0, m0), tag=free_banks.pop(0))
+                for m in range(per_bank):
+                    product(bank[:, m, :], w3_mx, m0 + m, z_mx, slice(0, width))
+                res = sb("res%d_%d" % (j0, m0), [P, per_bank, width], F32)
+                if last and m0 > 0:
+                    nc.vector.tensor_copy(out=res[:], in_=bank[:])
+                else:
+                    nc.scalar.copy(out=res[:], in_=bank[:])
+                nc.sync.dma_start(out=out_rows[:, m0 : m0 + per_bank, j0 : j0 + width], in_=res[:])

@@ -17,8 +17,10 @@ ACT = mybir.ActivationFunctionType
 
 P = 128
 PACK = 4
+LIST_ROWS = 16
+QUADRANT = 32
+HALF = H // 2
 CHUNK = 128
-W2_SPLIT = 256
 STRETCHES = [(0, 256), (256, 128), (384, 128)]
 
 
@@ -28,12 +30,12 @@ def tile_picked_maskdec_relu_p_kernel(tc, x_words, x_scales, w1, w2, w3, offs, m
         keep = ctx.enter_context(tc.tile_pool(name="keep", bufs=1))
         psum = ctx.enter_context(tc.psum_pool(name="psum", bufs=1))
 
-        def sb(name, shape, dtype, tag=None):
-            return keep.tile(shape, dtype, name=name, tag=tag or name, align_bytes=64)
+        def sb(name, shape, dtype, on=None):
+            return keep.tile(shape, dtype, name=name, tag=on or name, align_bytes=64)
 
-        offs_sb = sb("offs_sb", [P, S // 16], U16)
-        mix_sb = sb("mix_sb", [P, S // 16], U16)
-        al_sb = sb("al_sb", [P, S // 16], U16)
+        offs_sb = sb("offs_sb", [P, S // LIST_ROWS], U16)
+        mix_sb = sb("mix_sb", [P, S // LIST_ROWS], U16)
+        al_sb = sb("al_sb", [P, S // LIST_ROWS], U16)
         xw = sb("xw", [P, T], I32)
         xs = sb("xs", [P, T], U8)
         warm_in = sb("warm_in", [P, 8], F32)
@@ -48,29 +50,34 @@ def tile_picked_maskdec_relu_p_kernel(tc, x_words, x_scales, w1, w2, w3, offs, m
             nc.sync.dma_start(out=raw[:], in_=w[:, c0:c1].rearrange("(p j) c -> p j c", j=PACK))
             return raw
 
-        nc.sync.dma_start(out=xw[:], in_=x_words[0].rearrange("p c r -> p (c r)").bitcast(I32))
+        w2_left = load_rows("w2_left", w2, 0, HALF)
         nc.sync.dma_start(offs_sb[:], offs)
-        for q in range(4):
-            nc.sync.dma_start(out=xs[32 * q : 32 * q + 4, :].bitcast(I32), in_=x_scales[0, 4 * q : 4 * q + 4, :].bitcast(I32))
         nc.sync.dma_start(mix_sb[:], mix)
-        w2_left = load_rows("w2_left", w2, 0, W2_SPLIT)
-        w2_right = load_rows("w2_right", w2, W2_SPLIT, H)
+        for r in range(PACK):
+            nc.sync.dma_start(out=xs[r:P:QUADRANT, :].bitcast(I32), in_=x_scales[0, r : K // 32 : PACK, :].bitcast(I32))
+        nc.sync.dma_start(out=xw[:], in_=x_words[0].rearrange("p c r -> p (c r)").bitcast(I32))
+        w2_right = load_rows("w2_right", w2, HALF, H)
         nc.sync.dma_start(al_sb[:], al)
-        w1_raw = load_rows("w1_raw", w1, 0, H)
+        w1_left = load_rows("w1_left", w1, 0, HALF)
+        w1_right = load_rows("w1_right", w1, HALF, H)
         w3_raw = load_rows("w3_raw", w3, 0, N)
-
-        def dealt(grouped):
-            return grouped[:].rearrange("p (t m j) -> p m j t", t=PACK, j=PACK)
 
         def by_four(raw):
             return raw[:].rearrange("p j (m t) -> p m j t", t=PACK)
+
+        def dealt(grouped):
+            return grouped[:].rearrange("p (t m j) -> p m j t", t=PACK, j=PACK)
 
         def quantize(name, grouped, width, pieces):
             codes = sb(name + "_codes", [P, width], U32)
             scales = sb(name + "_scales", [P, width], U8)
             step = width // pieces
             for c0 in range(0, width, step):
-                nc.vector.quantize_mx(out=codes[:, c0 : c0 + step].bitcast(FP8X4), scales=scales[:, c0 : c0 + step], in_=grouped[:, PACK * c0 : PACK * (c0 + step)])
+                nc.vector.quantize_mx(
+                    out=codes[:, c0 : c0 + step].bitcast(FP8X4),
+                    scales=scales[:, c0 : c0 + step],
+                    in_=grouped[:, PACK * c0 : PACK * (c0 + step)],
+                )
             return codes, scales
 
         def product(dst, weights, m, moving, cols):
@@ -87,26 +94,31 @@ def tile_picked_maskdec_relu_p_kernel(tc, x_words, x_scales, w1, w2, w3, offs, m
         q_words = sb("q_words", [P, S], U32)
         q_scales = sb("q_scales", [P, S], U8)
         m_words = sb("m_words", [P, S], U32)
-        nc.vector.tensor_copy(out=q_words[:], in_=xw[:].bitcast(U32).indirect(offs_sb[:]))
+        m_scales = sb("m_scales", [P, S], U8)
         nc.vector.tensor_copy(out=q_scales[:], in_=xs[:].indirect(offs_sb[:]))
+        nc.vector.tensor_copy(out=m_scales[:], in_=xs[:].indirect(mix_sb[:]))
+        nc.vector.tensor_copy(out=q_words[:], in_=xw[:].bitcast(U32).indirect(offs_sb[:]))
         nc.vector.tensor_copy(out=m_words[:], in_=xw[:].bitcast(U32).indirect(mix_sb[:]))
 
         w2_bf = sb("w2_bf", [P, PACK * H], BF16)
-        nc.scalar.copy(out=dealt(w2_bf)[:, : W2_SPLIT // PACK], in_=by_four(w2_left))
-        nc.vector.tensor_copy(out=dealt(w2_bf)[:, W2_SPLIT // PACK :], in_=by_four(w2_right))
+        nc.scalar.copy(out=dealt(w2_bf)[:, : HALF // PACK], in_=by_four(w2_left))
+        nc.scalar.copy(out=dealt(w2_bf)[:, HALF // PACK :], in_=by_four(w2_right))
         w2_mx = quantize("w2", w2_bf, H, 2)
+        w1_bf = sb("w1_bf", [P, PACK * H], BF16)
+        nc.scalar.copy(out=dealt(w1_bf)[:, : HALF // PACK], in_=by_four(w1_left))
+
         s_sb = []
         for t in range(PACK):
-            bank = psum.tile([P, S], F32, name="s_bank%d" % t, tag="a%d" % t)
+            bank = psum.tile([P, S], F32, name="s_bank%d" % t, tag="s%d" % t)
             product(bank[:], w2_mx, t, (q_words, q_scales), slice(0, S))
-            s_t = sb("s_sb%d" % t, [P, S], F32)
-            nc.scalar.copy(out=s_t[:], in_=bank[:])
+            s_t = sb("s_sb%d" % t, [P, S], F32, on={1: "w1_right", 3: "w1_bf"}.get(t))
+            if t % 2 == 0:
+                nc.scalar.copy(out=s_t[:], in_=bank[:])
+            else:
+                nc.vector.tensor_copy(out=s_t[:], in_=bank[:])
             s_sb.append(s_t)
 
-        m_scales = sb("m_scales", [P, S], U8, tag="w2_bf")
-        nc.vector.tensor_copy(out=m_scales[:], in_=xs[:].indirect(mix_sb[:]))
-        w1_bf = sb("w1_bf", [P, PACK * H], BF16)
-        nc.vector.tensor_copy(out=dealt(w1_bf), in_=by_four(w1_raw))
+        nc.vector.tensor_copy(out=dealt(w1_bf)[:, HALF // PACK :], in_=by_four(w1_right))
         w1_mx = quantize("w1", w1_bf, H, 1)
         e_banks = []
         for c in range(S // CHUNK):
@@ -120,12 +132,14 @@ def tile_picked_maskdec_relu_p_kernel(tc, x_words, x_scales, w1, w2, w3, offs, m
         w3_mx = quantize("w3", w3_bf, N, 1)
 
         out_rows = out.rearrange("(m p) j -> p m j", p=P)
-        free_banks = ["a0", "a1", "a2", "a3", "e0"]
+        free_banks = ["s0", "s1", "s2", "s3", "e0"]
         for j0, width in STRETCHES:
-            mask = sb("mask%d" % j0, [P, PACK, width], F32)
+            mask = sb("mask%d" % j0, [P, PACK, width], F32, on={256: "m_words", 384: "w1_codes"}.get(j0))
             for t in range(PACK):
-                nc.scalar.activation(mask[:, t, :], s_sb[t][:].indirect(al_sb[:, j0 // 16 : (j0 + width) // 16]), ACT.Sigmoid)
-            z_bf = sb("z_bf%d" % j0, [P, width * PACK], BF16, tag="w3_bf")
+                entries = al_sb[:, j0 // LIST_ROWS : (j0 + width) // LIST_ROWS]
+                nc.scalar.activation(mask[:, t, :], s_sb[t][:].indirect(entries), ACT.Sigmoid)
+
+            z_bf = sb("z_bf%d" % j0, [P, width * PACK], BF16, on="w3_bf")
             for lo in range(0, width, CHUNK):
                 nc.vector.scalar_tensor_tensor(
                     out=z_bf[:, lo * PACK : (lo + CHUNK) * PACK].rearrange("p (n t) -> p n t", t=PACK),
@@ -136,6 +150,7 @@ def tile_picked_maskdec_relu_p_kernel(tc, x_words, x_scales, w1, w2, w3, offs, m
                     op1=ALU.mult,
                 )
             z_mx = quantize("z%d" % j0, z_bf, width, 1)
+
             last = j0 + width == S
             per_bank = 2 if last else S // width
             for m0 in range(0, N // P, per_bank):

@@ -21,7 +21,8 @@ LIST_ROWS = 16
 QUADRANT = 32
 HALF = H // 2
 CHUNK = 128
-STRETCHES = [(0, 256), (256, 128), (384, 128)]
+GROUPS = HALF // PACK
+SCALAR_GROUPS = 40
 
 
 def tile_picked_maskdec_relu_p_kernel(tc, x_words, x_scales, w1, w2, w3, offs, mix, al, out):
@@ -33,34 +34,10 @@ def tile_picked_maskdec_relu_p_kernel(tc, x_words, x_scales, w1, w2, w3, offs, m
         def sb(name, shape, dtype, on=None):
             return keep.tile(shape, dtype, name=name, tag=on or name, align_bytes=64)
 
-        offs_sb = sb("offs_sb", [P, S // LIST_ROWS], U16)
-        mix_sb = sb("mix_sb", [P, S // LIST_ROWS], U16)
-        al_sb = sb("al_sb", [P, S // LIST_ROWS], U16)
-        xw = sb("xw", [P, T], I32)
-        xs = sb("xs", [P, T], U8)
-        warm_in = sb("warm_in", [P, 8], F32)
-        warm_out = sb("warm_out", [P, 8], F32)
-
-        nc.vector.memset(xs[:].bitcast(I32), 0)
-        nc.vector.memset(warm_in[:], 0.0)
-        nc.scalar.activation(warm_out[:], warm_in[:], ACT.Sigmoid)
-
         def load_rows(name, w, c0, c1):
             raw = sb(name, [P, PACK, c1 - c0], F32)
             nc.sync.dma_start(out=raw[:], in_=w[:, c0:c1].rearrange("(p j) c -> p j c", j=PACK))
             return raw
-
-        w2_left = load_rows("w2_left", w2, 0, HALF)
-        nc.sync.dma_start(offs_sb[:], offs)
-        nc.sync.dma_start(mix_sb[:], mix)
-        for r in range(PACK):
-            nc.sync.dma_start(out=xs[r:P:QUADRANT, :].bitcast(I32), in_=x_scales[0, r : K // 32 : PACK, :].bitcast(I32))
-        nc.sync.dma_start(out=xw[:], in_=x_words[0].rearrange("p c r -> p (c r)").bitcast(I32))
-        w2_right = load_rows("w2_right", w2, HALF, H)
-        nc.sync.dma_start(al_sb[:], al)
-        w1_left = load_rows("w1_left", w1, 0, HALF)
-        w1_right = load_rows("w1_right", w1, HALF, H)
-        w3_raw = load_rows("w3_raw", w3, 0, N)
 
         def by_four(raw):
             return raw[:].rearrange("p j (m t) -> p m j t", t=PACK)
@@ -68,17 +45,18 @@ def tile_picked_maskdec_relu_p_kernel(tc, x_words, x_scales, w1, w2, w3, offs, m
         def dealt(grouped):
             return grouped[:].rearrange("p (t m j) -> p m j t", t=PACK, j=PACK)
 
-        def quantize(name, grouped, width, pieces):
-            codes = sb(name + "_codes", [P, width], U32)
-            scales = sb(name + "_scales", [P, width], U8)
-            step = width // pieces
-            for c0 in range(0, width, step):
-                nc.vector.quantize_mx(
-                    out=codes[:, c0 : c0 + step].bitcast(FP8X4),
-                    scales=scales[:, c0 : c0 + step],
-                    in_=grouped[:, PACK * c0 : PACK * (c0 + step)],
-                )
-            return codes, scales
+        def in_order(grouped):
+            return grouped[:].rearrange("p (m t j) -> p m j t", t=PACK, j=PACK)
+
+        def mx_tiles(name, width):
+            return sb(name + "_codes", [P, width], U32), sb(name + "_scales", [P, width], U8)
+
+        def quantize(mx, grouped, c0, c1):
+            nc.vector.quantize_mx(
+                out=mx[0][:, c0:c1].bitcast(FP8X4),
+                scales=mx[1][:, c0:c1],
+                in_=grouped[:, PACK * c0 : PACK * c1],
+            )
 
         def product(dst, weights, m, moving, cols):
             nc.tensor.matmul_mx(
@@ -91,35 +69,70 @@ def tile_picked_maskdec_relu_p_kernel(tc, x_words, x_scales, w1, w2, w3, offs, m
                 stop=True,
             )
 
+        shared = ctx.enter_context(tc.tile_pool(name="shared", bufs=1))
+        offs_sb = sb("offs_sb", [P, S // LIST_ROWS], U16)
+        mix_sb = sb("mix_sb", [P, S // LIST_ROWS], U16)
+        al_sb = sb("al_sb", [P, S // LIST_ROWS], U16)
+        xw = sb("xw", [P, T], I32)
+        xs = sb("xs", [P, T], U8)
+        warm_in = sb("warm_in", [P, 8], F32)
+        warm_out = sb("warm_out", [P, 8], F32)
+
+        nc.vector.memset(xs[:].bitcast(I32), 0)
+        nc.vector.memset(warm_in[:], 0.0)
+        nc.scalar.activation(warm_out[:], warm_in[:], ACT.Sigmoid)
+
+        w2_left = load_rows("w2_left", w2, 0, HALF)
+        nc.sync.dma_start(offs_sb[:], offs)
+        nc.sync.dma_start(mix_sb[:], mix)
+        for r in range(PACK):
+            nc.sync.dma_start(out=xs[r:P:QUADRANT, :].bitcast(I32), in_=x_scales[0, r : K // 32 : PACK, :].bitcast(I32))
+        nc.sync.dma_start(out=xw[:], in_=x_words[0].rearrange("p c r -> p (c r)").bitcast(I32))
+        w2_right = load_rows("w2_right", w2, HALF, H)
+        w1_left = load_rows("w1_left", w1, 0, HALF)
+        w1_right = load_rows("w1_right", w1, HALF, H)
+        nc.sync.dma_start(al_sb[:], al)
+        w3_raw = shared.tile([P, PACK, N], F32, name="w3_raw", offset=8192, align_bytes=64)
+        nc.sync.dma_start(out=w3_raw[:], in_=w3.rearrange("(p j) c -> p j c", j=PACK))
+
         q_words = sb("q_words", [P, S], U32)
         q_scales = sb("q_scales", [P, S], U8)
-        m_words = sb("m_words", [P, S], U32)
         m_scales = sb("m_scales", [P, S], U8)
         nc.vector.tensor_copy(out=q_scales[:], in_=xs[:].indirect(offs_sb[:]))
         nc.vector.tensor_copy(out=m_scales[:], in_=xs[:].indirect(mix_sb[:]))
         nc.vector.tensor_copy(out=q_words[:], in_=xw[:].bitcast(U32).indirect(offs_sb[:]))
-        nc.vector.tensor_copy(out=m_words[:], in_=xw[:].bitcast(U32).indirect(mix_sb[:]))
 
         w2_bf = sb("w2_bf", [P, PACK * H], BF16)
-        nc.scalar.copy(out=dealt(w2_bf)[:, : HALF // PACK], in_=by_four(w2_left))
-        nc.scalar.copy(out=dealt(w2_bf)[:, HALF // PACK :], in_=by_four(w2_right))
-        w2_mx = quantize("w2", w2_bf, H, 2)
-        w1_bf = sb("w1_bf", [P, PACK * H], BF16)
-        nc.scalar.copy(out=dealt(w1_bf)[:, : HALF // PACK], in_=by_four(w1_left))
+        split = GROUPS + SCALAR_GROUPS
+        nc.scalar.copy(out=dealt(w2_bf)[:, :GROUPS], in_=by_four(w2_left))
+        nc.scalar.copy(out=dealt(w2_bf)[:, GROUPS:split], in_=by_four(w2_right)[:, :SCALAR_GROUPS])
+        nc.vector.tensor_copy(out=dealt(w2_bf)[:, split:], in_=by_four(w2_right)[:, SCALAR_GROUPS:])
+        w2_mx = mx_tiles("w2", H)
+        quantize(w2_mx, w2_bf, 0, HALF)
+        quantize(w2_mx, w2_bf, HALF, H)
+        m_words = sb("m_words", [P, S], U32, on="w2_bf")
+        nc.vector.tensor_copy(out=m_words[:], in_=xw[:].bitcast(U32).indirect(mix_sb[:]))
 
-        s_sb = []
+        w1_bf = shared.tile([P, PACK * H], BF16, name="w1_bf", offset=1024, align_bytes=64)
+        nc.scalar.copy(out=dealt(w1_bf)[:, :GROUPS], in_=by_four(w1_left))
+        s_banks = []
         for t in range(PACK):
             bank = psum.tile([P, S], F32, name="s_bank%d" % t, tag="s%d" % t)
             product(bank[:], w2_mx, t, (q_words, q_scales), slice(0, S))
-            s_t = sb("s_sb%d" % t, [P, S], F32, on={1: "w1_right", 3: "w1_bf"}.get(t))
-            if t % 2 == 0:
-                nc.scalar.copy(out=s_t[:], in_=bank[:])
-            else:
-                nc.vector.tensor_copy(out=s_t[:], in_=bank[:])
+            s_banks.append(bank)
+        s_sb = []
+        for t in range(PACK - 1):
+            s_t = sb("s_sb%d" % t, [P, S], F32)
+            nc.scalar.copy(out=s_t[:], in_=s_banks[t][:])
             s_sb.append(s_t)
 
-        nc.vector.tensor_copy(out=dealt(w1_bf)[:, HALF // PACK :], in_=by_four(w1_right))
-        w1_mx = quantize("w1", w1_bf, H, 1)
+        nc.vector.tensor_copy(out=dealt(w1_bf)[:, GROUPS:], in_=by_four(w1_right))
+        w1_mx = mx_tiles("w1", H)
+        quantize(w1_mx, w1_bf, 0, H)
+        for t in (3,):
+            s_t = shared.tile([P, S], F32, name="s_sb%d" % t, offset=0, align_bytes=64)
+            nc.vector.tensor_copy(out=s_t[:], in_=s_banks[t][:])
+            s_sb.append(s_t)
         e_banks = []
         for c in range(S // CHUNK):
             bank = psum.tile([P, PACK, CHUNK], F32, name="e_bank%d" % c, tag="e%d" % c)
@@ -127,39 +140,74 @@ def tile_picked_maskdec_relu_p_kernel(tc, x_words, x_scales, w1, w2, w3, offs, m
                 product(bank[:, t, :], w1_mx, t, (m_words, m_scales), slice(c * CHUNK, (c + 1) * CHUNK))
             e_banks.append(bank)
 
-        w3_bf = sb("w3_bf", [P, PACK * N], BF16)
-        nc.vector.tensor_copy(out=w3_bf[:].rearrange("p (m i j) -> p m j i", i=PACK, j=PACK), in_=by_four(w3_raw))
-        w3_mx = quantize("w3", w3_bf, N, 1)
+        w3_mx = mx_tiles("w3", N)
+        w3_bf = []
+        for h in range(2):
+            half = shared.tile([P, PACK * HALF], BF16, name="w3_bf%d" % h, offset=2048 + 2048 * h, align_bytes=64)
+            nc.vector.tensor_copy(out=in_order(half), in_=by_four(w3_raw)[:, h * GROUPS : (h + 1) * GROUPS])
+            w3_bf.append(half)
+        for h in range(2):
+            nc.vector.quantize_mx(
+                out=w3_mx[0][:, h * HALF : (h + 1) * HALF].bitcast(FP8X4),
+                scales=w3_mx[1][:, h * HALF : (h + 1) * HALF],
+                in_=w3_bf[h][:],
+            )
 
-        out_rows = out.rearrange("(m p) j -> p m j", p=P)
-        free_banks = ["s0", "s1", "s2", "s3", "e0"]
-        for j0, width in STRETCHES:
-            mask = sb("mask%d" % j0, [P, PACK, width], F32, on={256: "m_words", 384: "w1_codes"}.get(j0))
+        def look_up(mask, first, lo, width):
+            entries = al_sb[:, (first + lo) // LIST_ROWS : (first + lo + width) // LIST_ROWS]
             for t in range(PACK):
-                entries = al_sb[:, j0 // LIST_ROWS : (j0 + width) // LIST_ROWS]
-                nc.scalar.activation(mask[:, t, :], s_sb[t][:].indirect(entries), ACT.Sigmoid)
+                nc.scalar.activation(mask[:, t, lo : lo + width], s_sb[t][:].indirect(entries), ACT.Sigmoid)
 
-            z_bf = sb("z_bf%d" % j0, [P, width * PACK], BF16, on="w3_bf")
-            for lo in range(0, width, CHUNK):
-                nc.vector.scalar_tensor_tensor(
-                    out=z_bf[:, lo * PACK : (lo + CHUNK) * PACK].rearrange("p (n t) -> p n t", t=PACK),
-                    in0=e_banks[(j0 + lo) // CHUNK][:].rearrange("p t n -> p n t"),
-                    scalar=0.0,
-                    in1=mask[:, :, lo : lo + CHUNK].rearrange("p t n -> p n t"),
-                    op0=ALU.max,
-                    op1=ALU.mult,
-                )
-            z_mx = quantize("z%d" % j0, z_bf, width, 1)
+        mask_early = sb("mask_early", [P, PACK, 2 * CHUNK], F32)
+        mask_late = [shared.tile([P, PACK, CHUNK], F32, name="mask%d" % c, offset=8192 + c * 2048, align_bytes=64) for c in range(2)]
+        look_up(mask_early, 0, 0, 2 * CHUNK)
+        look_up(mask_late[0], 2 * CHUNK, 0, CHUNK)
+        look_up(mask_late[1], 3 * CHUNK, 0, CHUNK)
 
-            last = j0 + width == S
-            per_bank = 2 if last else S // width
-            for m0 in range(0, N // P, per_bank):
-                bank = psum.tile([P, per_bank, width], F32, name="o_bank%d_%d" % (j0, m0), tag=free_banks.pop(0))
-                for m in range(per_bank):
-                    product(bank[:, m, :], w3_mx, m0 + m, z_mx, slice(0, width))
-                res = sb("res%d_%d" % (j0, m0), [P, per_bank, width], F32)
-                if last and m0 > 0:
-                    nc.vector.tensor_copy(out=res[:], in_=bank[:])
-                else:
-                    nc.scalar.copy(out=res[:], in_=bank[:])
-                nc.sync.dma_start(out=out_rows[:, m0 : m0 + per_bank, j0 : j0 + width], in_=res[:])
+        z_bf = shared.tile([P, PACK * 2 * CHUNK], BF16, name="z_bf", offset=2048, align_bytes=64)
+        z_mx = [mx_tiles("z%d" % c, CHUNK) for c in range(S // CHUNK)]
+        out_rows = out.rearrange("(m p) j -> p m j", p=P)
+
+        def masked(c, dst):
+            mask = mask_early if c < 2 else mask_late[c - 2]
+            lo = c * CHUNK if c < 2 else 0
+            nc.vector.scalar_tensor_tensor(
+                out=dst.rearrange("p (n t) -> p n t", t=PACK),
+                in0=e_banks[c][:].rearrange("p t n -> p n t"),
+                scalar=0.0,
+                in1=mask[:, :, lo : lo + CHUNK].rearrange("p t n -> p n t"),
+                op0=ALU.max,
+                op1=ALU.mult,
+            )
+
+        def z_of(c):
+            return z_bf[:, c % 2 * PACK * CHUNK : (c % 2 + 1) * PACK * CHUNK]
+
+        def decode(c, m0, count, tag):
+            bank = psum.tile([P, count, CHUNK], F32, name="o_bank%d_%d" % (c, m0), tag=tag)
+            for m in range(count):
+                product(bank[:, m, :], w3_mx, m0 + m, z_mx[c], slice(0, CHUNK))
+            return bank
+
+        def leave(c, m0, count, bank, copy):
+            res = sb("res%d_%d" % (c, m0), [P, count, CHUNK], F32)
+            copy(out=res[:], in_=bank[:])
+            nc.sync.dma_start(out=out_rows[:, m0 : m0 + count, c * CHUNK : (c + 1) * CHUNK], in_=res[:])
+
+        masked(0, z_of(0))
+        masked(1, z_of(1))
+        quantize(z_mx[0], z_of(0), 0, CHUNK)
+        quantize(z_mx[1], z_of(1), 0, CHUNK)
+        bank0 = decode(0, 0, PACK, "s0")
+        bank1 = decode(1, 0, PACK, "s1")
+        masked(2, z_of(2))
+        leave(0, 0, PACK, bank0, nc.vector.tensor_copy)
+        quantize(z_mx[2], z_of(2), 0, CHUNK)
+        bank2 = decode(2, 0, PACK, "s2")
+        z_last = sb("z_last", [P, PACK * CHUNK], BF16, on="z1_codes")
+        masked(3, z_last[:])
+        quantize(z_mx[3], z_last, 0, CHUNK)
+        leave(1, 0, PACK, bank1, nc.scalar.copy)
+        leave(2, 0, PACK, bank2, nc.scalar.copy)
+        leave(3, 0, 2, decode(3, 0, 2, "s3"), nc.scalar.copy)
+        leave(3, 2, 2, decode(3, 2, 2, "e0"), nc.vector.tensor_copy)

@@ -113,26 +113,20 @@ def tile_picked_maskdec_relu_p_kernel(tc, x_words, x_scales, w1, w2, w3, offs, m
         m_words = sb("m_words", [P, S], U32, on="w2_bf")
         nc.vector.tensor_copy(out=m_words[:], in_=xw[:].bitcast(U32).indirect(mix_sb[:]))
 
-        w1_bf = shared.tile([P, PACK * H], BF16, name="w1_bf", offset=1024, align_bytes=64)
+        w1_bf = shared.tile([P, PACK * H], BF16, name="w1_bf", offset=16384, align_bytes=64)
         nc.scalar.copy(out=dealt(w1_bf)[:, :GROUPS], in_=by_four(w1_left))
         s_banks = []
         for t in range(PACK):
             bank = psum.tile([P, S], F32, name="s_bank%d" % t, tag="s%d" % t)
             product(bank[:], w2_mx, t, (q_words, q_scales), slice(0, S))
             s_banks.append(bank)
-        s_sb = []
-        for t in range(PACK - 1):
-            s_t = sb("s_sb%d" % t, [P, S], F32)
-            nc.scalar.copy(out=s_t[:], in_=s_banks[t][:])
-            s_sb.append(s_t)
-
         nc.vector.tensor_copy(out=dealt(w1_bf)[:, GROUPS:], in_=by_four(w1_right))
+        s_sb = [sb("s_sb%d" % t, [P, S], F32, on={3: "w1_right"}.get(t)) for t in range(PACK)]
+        for t in range(PACK - 1):
+            nc.scalar.copy(out=s_sb[t][:], in_=s_banks[t][:])
+        nc.vector.tensor_copy(out=s_sb[3][:], in_=s_banks[3][:])
         w1_mx = mx_tiles("w1", H)
         quantize(w1_mx, w1_bf, 0, H)
-        for t in (3,):
-            s_t = shared.tile([P, S], F32, name="s_sb%d" % t, offset=0, align_bytes=64)
-            nc.vector.tensor_copy(out=s_t[:], in_=s_banks[t][:])
-            s_sb.append(s_t)
         e_banks = []
         for c in range(S // CHUNK):
             bank = psum.tile([P, PACK, CHUNK], F32, name="e_bank%d" % c, tag="e%d" % c)

@@ -22,7 +22,7 @@ QUADRANT = 32
 HALF = H // 2
 CHUNK = 128
 GROUPS = HALF // PACK
-SCALAR_GROUPS = 40
+EARLY = 192
 
 
 def tile_picked_maskdec_relu_p_kernel(tc, x_words, x_scales, w1, w2, w3, offs, mix, al, out):
@@ -84,13 +84,13 @@ def tile_picked_maskdec_relu_p_kernel(tc, x_words, x_scales, w1, w2, w3, offs, m
 
         w2_left = load_rows("w2_left", w2, 0, HALF)
         nc.sync.dma_start(offs_sb[:], offs)
-        nc.sync.dma_start(mix_sb[:], mix)
         for r in range(PACK):
             nc.sync.dma_start(out=xs[r:P:QUADRANT, :].bitcast(I32), in_=x_scales[0, r : K // 32 : PACK, :].bitcast(I32))
+        nc.sync.dma_start(mix_sb[:], mix)
         nc.sync.dma_start(out=xw[:], in_=x_words[0].rearrange("p c r -> p (c r)").bitcast(I32))
         w2_right = load_rows("w2_right", w2, HALF, H)
-        w1_left = load_rows("w1_left", w1, 0, HALF)
-        w1_right = load_rows("w1_right", w1, HALF, H)
+        w1_left = load_rows("w1_left", w1, 0, EARLY)
+        w1_right = load_rows("w1_right", w1, EARLY, H)
         nc.sync.dma_start(al_sb[:], al)
         w3_raw = shared.tile([P, PACK, N], F32, name="w3_raw", offset=8192, align_bytes=64)
         nc.sync.dma_start(out=w3_raw[:], in_=w3.rearrange("(p j) c -> p j c", j=PACK))
@@ -102,27 +102,44 @@ def tile_picked_maskdec_relu_p_kernel(tc, x_words, x_scales, w1, w2, w3, offs, m
         nc.vector.tensor_copy(out=m_scales[:], in_=xs[:].indirect(mix_sb[:]))
         nc.vector.tensor_copy(out=q_words[:], in_=xw[:].bitcast(U32).indirect(offs_sb[:]))
 
-        w2_bf = sb("w2_bf", [P, PACK * H], BF16)
-        split = GROUPS + SCALAR_GROUPS
-        nc.scalar.copy(out=dealt(w2_bf)[:, :GROUPS], in_=by_four(w2_left))
-        nc.scalar.copy(out=dealt(w2_bf)[:, GROUPS:split], in_=by_four(w2_right)[:, :SCALAR_GROUPS])
-        nc.vector.tensor_copy(out=dealt(w2_bf)[:, split:], in_=by_four(w2_right)[:, SCALAR_GROUPS:])
+        def two_planes(raw, u):
+            return by_four(raw)[:, :, :, 2 * u : 2 * u + 2]
+
+        def dealt_pair(grouped):
+            return grouped[:].rearrange("p (t m j) -> p m j t", t=2, j=PACK)
+
+        w2_bf = [sb("w2_bf%d" % u, [P, PACK * HALF], BF16) for u in range(2)]
+        for u in range(2):
+            nc.scalar.copy(out=dealt_pair(w2_bf[u])[:, :GROUPS], in_=two_planes(w2_left, u))
+        nc.vector.tensor_copy(out=dealt_pair(w2_bf[0])[:, GROUPS:], in_=two_planes(w2_right, 0))
+        nc.scalar.copy(out=dealt_pair(w2_bf[1])[:, GROUPS:], in_=two_planes(w2_right, 1))
         w2_mx = mx_tiles("w2", H)
-        quantize(w2_mx, w2_bf, 0, HALF)
-        quantize(w2_mx, w2_bf, HALF, H)
-        m_words = sb("m_words", [P, S], U32, on="w2_bf")
+        for u, lo, hi in ((0, 0, P), (0, P, HALF), (1, 0, HALF)):
+            nc.vector.quantize_mx(
+                out=w2_mx[0][:, u * HALF + lo : u * HALF + hi].bitcast(FP8X4),
+                scales=w2_mx[1][:, u * HALF + lo : u * HALF + hi],
+                in_=w2_bf[u][:, PACK * lo : PACK * hi],
+            )
+        m_words = sb("m_words", [P, S], U32, on="w2_bf0")
         nc.vector.tensor_copy(out=m_words[:], in_=xw[:].bitcast(U32).indirect(mix_sb[:]))
 
         w1_bf = shared.tile([P, PACK * H], BF16, name="w1_bf", offset=16384, align_bytes=64)
-        nc.scalar.copy(out=dealt(w1_bf)[:, :GROUPS], in_=by_four(w1_left))
-        s_banks = []
-        for t in range(PACK):
+        nc.scalar.copy(out=dealt(w1_bf)[:, : EARLY // PACK], in_=by_four(w1_left))
+        first = []
+        for h, tag in enumerate(("s0", "e3")):
+            bank = psum.tile([P, HALF], F32, name="s_first%d" % h, tag=tag)
+            product(bank[:], w2_mx, 0, (q_words, q_scales), slice(h * HALF, (h + 1) * HALF))
+            first.append(bank)
+        s_banks = [None]
+        for t in range(1, PACK):
             bank = psum.tile([P, S], F32, name="s_bank%d" % t, tag="s%d" % t)
             product(bank[:], w2_mx, t, (q_words, q_scales), slice(0, S))
             s_banks.append(bank)
-        nc.vector.tensor_copy(out=dealt(w1_bf)[:, GROUPS:], in_=by_four(w1_right))
+        nc.vector.tensor_copy(out=dealt(w1_bf)[:, EARLY // PACK :], in_=by_four(w1_right))
         s_sb = [sb("s_sb%d" % t, [P, S], F32, on={3: "w1_right"}.get(t)) for t in range(PACK)]
-        for t in range(PACK - 1):
+        for h in range(2):
+            nc.scalar.copy(out=s_sb[0][:, h * HALF : (h + 1) * HALF], in_=first[h][:])
+        for t in range(1, PACK - 1):
             nc.scalar.copy(out=s_sb[t][:], in_=s_banks[t][:])
         nc.vector.tensor_copy(out=s_sb[3][:], in_=s_banks[3][:])
         w1_mx = mx_tiles("w1", H)

@@ -82,13 +82,16 @@ def tile_picked_maskdec_relu_p_kernel(tc, x_words, x_scales, w1, w2, w3, offs, m
         nc.vector.memset(warm_in[:], 0.0)
         nc.scalar.activation(warm_out[:], warm_in[:], ACT.Sigmoid)
 
-        w2_left = load_rows("w2_left", w2, 0, HALF)
+        w2_pairs = w2.rearrange("(p u j) c -> p u j c", u=2, j=2)
+        w2_left = sb("w2_left", [P, 2, H], F32)
+        nc.sync.dma_start(out=w2_left[:], in_=w2_pairs[:, 0])
         nc.sync.dma_start(offs_sb[:], offs)
         for r in range(PACK):
             nc.sync.dma_start(out=xs[r:P:QUADRANT, :].bitcast(I32), in_=x_scales[0, r : K // 32 : PACK, :].bitcast(I32))
         nc.sync.dma_start(mix_sb[:], mix)
         nc.sync.dma_start(out=xw[:], in_=x_words[0].rearrange("p c r -> p (c r)").bitcast(I32))
-        w2_right = load_rows("w2_right", w2, HALF, H)
+        w2_right = sb("w2_right", [P, 2, H], F32)
+        nc.sync.dma_start(out=w2_right[:], in_=w2_pairs[:, 1])
         w1_left = load_rows("w1_left", w1, 0, EARLY)
         w1_right = load_rows("w1_right", w1, EARLY, H)
         nc.sync.dma_start(al_sb[:], al)
@@ -110,9 +113,9 @@ def tile_picked_maskdec_relu_p_kernel(tc, x_words, x_scales, w1, w2, w3, offs, m
 
         w2_bf = [sb("w2_bf%d" % u, [P, PACK * HALF], BF16) for u in range(2)]
         for u in range(2):
-            nc.scalar.copy(out=dealt_pair(w2_bf[u])[:, :GROUPS], in_=two_planes(w2_left, u))
-        nc.vector.tensor_copy(out=dealt_pair(w2_bf[0])[:, GROUPS:], in_=two_planes(w2_right, 0))
-        nc.scalar.copy(out=dealt_pair(w2_bf[1])[:, GROUPS:], in_=two_planes(w2_right, 1))
+            nc.scalar.copy(out=dealt_pair(w2_bf[u])[:, :, 0:2], in_=two_planes(w2_left, u))
+        nc.vector.tensor_copy(out=dealt_pair(w2_bf[0])[:, :, 2:4], in_=two_planes(w2_right, 0))
+        nc.scalar.copy(out=dealt_pair(w2_bf[1])[:, :, 2:4], in_=two_planes(w2_right, 1))
         w2_mx = mx_tiles("w2", H)
         for u, lo, hi in ((0, 0, P), (0, P, HALF), (1, 0, HALF)):
             nc.vector.quantize_mx(

@@ -19,6 +19,7 @@ P = 128
 PACK = 4
 LIST_ROWS = 16
 QUADRANT = 32
+BLOCK = 8
 HALF = H // 2
 CHUNK = 128
 GROUPS = HALF // PACK
@@ -79,30 +80,39 @@ def tile_picked_maskdec_relu_p_kernel(tc, x_words, x_scales, w1, w2, w3, offs, m
         warm_out = sb("warm_out", [P, 8], F32)
 
         nc.vector.memset(xs[:].bitcast(I32), 0)
+        q_scales = sb("q_scales", [P, S], U8)
+        m_scales = sb("m_scales", [P, S], U8)
         nc.vector.memset(warm_in[:], 0.0)
+        nc.vector.memset(q_scales[:].bitcast(I32), 0)
+        nc.vector.memset(m_scales[:].bitcast(I32), 0)
         nc.scalar.activation(warm_out[:], warm_in[:], ACT.Sigmoid)
 
         w2_pairs = w2.rearrange("(p u j) c -> p u j c", u=2, j=2)
         w2_left = sb("w2_left", [P, 2, H], F32)
         nc.sync.dma_start(out=w2_left[:], in_=w2_pairs[:, 0])
         nc.sync.dma_start(offs_sb[:], offs)
-        for r in range(PACK):
-            nc.sync.dma_start(out=xs[r:P:QUADRANT, :].bitcast(I32), in_=x_scales[0, r : K // 32 : PACK, :].bitcast(I32))
         nc.sync.dma_start(mix_sb[:], mix)
+        nc.sync.dma_start(out=xs[0:P:BLOCK, :].bitcast(I32), in_=x_scales[0].bitcast(I32))
         nc.sync.dma_start(out=xw[:], in_=x_words[0].rearrange("p c r -> p (c r)").bitcast(I32))
         w2_right = sb("w2_right", [P, 2, H], F32)
         nc.sync.dma_start(out=w2_right[:], in_=w2_pairs[:, 1])
         w1_left = load_rows("w1_left", w1, 0, EARLY)
+
+        def place(scales, picked):
+            for r in range(PACK):
+                nc.sync.dma_start(out=scales[r:P:QUADRANT, :].bitcast(I32), in_=picked[BLOCK * r : P : QUADRANT, :].bitcast(I32))
+
+        q_words = sb("q_words", [P, S], U32)
+        q_picked = sb("q_picked", [P, S], U8)
+        m_picked = sb("m_picked", [P, S], U8)
+        nc.vector.tensor_copy(out=q_picked[:], in_=xs[:].indirect(offs_sb[:]))
+        nc.vector.tensor_copy(out=m_picked[:], in_=xs[:].indirect(mix_sb[:]))
+        place(q_scales, q_picked)
         w1_right = load_rows("w1_right", w1, EARLY, H)
         nc.sync.dma_start(al_sb[:], al)
         w3_raw = shared.tile([P, PACK, N], F32, name="w3_raw", offset=8192, align_bytes=64)
         nc.sync.dma_start(out=w3_raw[:], in_=w3.rearrange("(p j) c -> p j c", j=PACK))
-
-        q_words = sb("q_words", [P, S], U32)
-        q_scales = sb("q_scales", [P, S], U8)
-        m_scales = sb("m_scales", [P, S], U8)
-        nc.vector.tensor_copy(out=q_scales[:], in_=xs[:].indirect(offs_sb[:]))
-        nc.vector.tensor_copy(out=m_scales[:], in_=xs[:].indirect(mix_sb[:]))
+        place(m_scales, m_picked)
         nc.vector.tensor_copy(out=q_words[:], in_=xw[:].bitcast(U32).indirect(offs_sb[:]))
 
         def two_planes(raw, u):

@@ -23,7 +23,7 @@ BLOCK = 8
 HALF = H // 2
 CHUNK = 128
 GROUPS = HALF // PACK
-EARLY = 192
+EARLY = 128
 
 
 def tile_picked_maskdec_relu_p_kernel(tc, x_words, x_scales, w1, w2, w3, offs, mix, al, out):
@@ -88,12 +88,13 @@ def tile_picked_maskdec_relu_p_kernel(tc, x_words, x_scales, w1, w2, w3, offs, m
         nc.scalar.activation(warm_out[:], warm_in[:], ACT.Sigmoid)
 
         w2_pairs = w2.rearrange("(p u j) c -> p u j c", u=2, j=2)
-        w2_left = sb("w2_left", [P, 2, H], F32)
-        nc.sync.dma_start(out=w2_left[:], in_=w2_pairs[:, 0])
+        w2_left = [sb("w2_left%d" % h, [P, 2, HALF], F32) for h in range(2)]
+        nc.sync.dma_start(out=w2_left[0][:], in_=w2_pairs[:, 0, :, :HALF])
         nc.sync.dma_start(offs_sb[:], offs)
         nc.sync.dma_start(mix_sb[:], mix)
         nc.sync.dma_start(out=xs[0:P:BLOCK, :].bitcast(I32), in_=x_scales[0].bitcast(I32))
         nc.sync.dma_start(out=xw[:], in_=x_words[0].rearrange("p c r -> p (c r)").bitcast(I32))
+        nc.sync.dma_start(out=w2_left[1][:], in_=w2_pairs[:, 0, :, HALF:])
         w2_right = sb("w2_right", [P, 2, H], F32)
         nc.sync.dma_start(out=w2_right[:], in_=w2_pairs[:, 1])
         w1_left = load_rows("w1_left", w1, 0, EARLY)
@@ -122,9 +123,11 @@ def tile_picked_maskdec_relu_p_kernel(tc, x_words, x_scales, w1, w2, w3, offs, m
             return grouped[:].rearrange("p (t m j) -> p m j t", t=2, j=PACK)
 
         w2_bf = [sb("w2_bf%d" % u, [P, PACK * HALF], BF16) for u in range(2)]
-        for u in range(2):
-            nc.scalar.copy(out=dealt_pair(w2_bf[u])[:, :, 0:2], in_=two_planes(w2_left, u))
-        nc.vector.tensor_copy(out=dealt_pair(w2_bf[0])[:, :, 2:4], in_=two_planes(w2_right, 0))
+        for h in range(2):
+            for u in range(2):
+                nc.scalar.copy(out=dealt_pair(w2_bf[u])[:, h * GROUPS : (h + 1) * GROUPS, 0:2], in_=two_planes(w2_left[h], u))
+        for t in range(2):
+            nc.vector.tensor_copy(out=dealt_pair(w2_bf[0])[:, :, 2:4, t], in_=by_four(w2_right)[:, :, :, t])
         nc.scalar.copy(out=dealt_pair(w2_bf[1])[:, :, 2:4], in_=two_planes(w2_right, 1))
         w2_mx = mx_tiles("w2", H)
         for u, lo, hi in ((0, 0, P), (0, P, HALF), (1, 0, HALF)):
@@ -133,9 +136,9 @@ def tile_picked_maskdec_relu_p_kernel(tc, x_words, x_scales, w1, w2, w3, offs, m
                 scales=w2_mx[1][:, u * HALF + lo : u * HALF + hi],
                 in_=w2_bf[u][:, PACK * lo : PACK * hi],
             )
+
         m_words = sb("m_words", [P, S], U32, on="w2_bf0")
         nc.vector.tensor_copy(out=m_words[:], in_=xw[:].bitcast(U32).indirect(mix_sb[:]))
-
         w1_bf = shared.tile([P, PACK * H], BF16, name="w1_bf", offset=16384, align_bytes=64)
         nc.scalar.copy(out=dealt(w1_bf)[:, : EARLY // PACK], in_=by_four(w1_left))
         first = []
@@ -183,7 +186,7 @@ def tile_picked_maskdec_relu_p_kernel(tc, x_words, x_scales, w1, w2, w3, offs, m
                 nc.scalar.activation(mask[:, t, lo : lo + width], s_sb[t][:].indirect(entries), ACT.Sigmoid)
 
         mask_early = sb("mask_early", [P, PACK, 2 * CHUNK], F32)
-        mask_late = [shared.tile([P, PACK, CHUNK], F32, name="mask%d" % c, offset=8192 + c * 2048, align_bytes=64) for c in range(2)]
+        mask_late = [shared.tile([P, PACK, CHUNK], F32, name="mask%d" % c, offset=16384 + c * 2048, align_bytes=64) for c in range(2)]
         look_up(mask_early, 0, 0, 2 * CHUNK)
         look_up(mask_late[0], 2 * CHUNK, 0, CHUNK)
         look_up(mask_late[1], 3 * CHUNK, 0, CHUNK)
@@ -222,16 +225,17 @@ def tile_picked_maskdec_relu_p_kernel(tc, x_words, x_scales, w1, w2, w3, offs, m
         masked(1, z_of(1))
         quantize(z_mx[0], z_of(0), 0, CHUNK)
         quantize(z_mx[1], z_of(1), 0, CHUNK)
-        bank0 = decode(0, 0, PACK, "s0")
+        bank0 = [decode(0, 0, 2, "s0"), decode(0, 2, 2, "s3")]
         bank1 = decode(1, 0, PACK, "s1")
         masked(2, z_of(2))
-        leave(0, 0, PACK, bank0, nc.vector.tensor_copy)
+        leave(0, 0, 2, bank0[0], nc.vector.tensor_copy)
         quantize(z_mx[2], z_of(2), 0, CHUNK)
         bank2 = decode(2, 0, PACK, "s2")
         z_last = sb("z_last", [P, PACK * CHUNK], BF16, on="z1_codes")
         masked(3, z_last[:])
         quantize(z_mx[3], z_last, 0, CHUNK)
+        leave(0, 2, 2, bank0[1], nc.scalar.copy)
         leave(1, 0, PACK, bank1, nc.scalar.copy)
         leave(2, 0, PACK, bank2, nc.scalar.copy)
-        leave(3, 0, 2, decode(3, 0, 2, "s3"), nc.scalar.copy)
+        leave(3, 0, 2, decode(3, 0, 2, "e1"), nc.scalar.copy)
         leave(3, 2, 2, decode(3, 2, 2, "e0"), nc.vector.tensor_copy)

@@ -23,7 +23,6 @@ BLOCK = 8
 HALF = H // 2
 CHUNK = 128
 GROUPS = HALF // PACK
-EARLY = 128
 
 
 def tile_picked_maskdec_relu_p_kernel(tc, x_words, x_scales, w1, w2, w3, offs, mix, al, out):
@@ -34,11 +33,6 @@ def tile_picked_maskdec_relu_p_kernel(tc, x_words, x_scales, w1, w2, w3, offs, m
 
         def sb(name, shape, dtype, on=None):
             return keep.tile(shape, dtype, name=name, tag=on or name, align_bytes=64)
-
-        def load_rows(name, w, c0, c1):
-            raw = sb(name, [P, PACK, c1 - c0], F32)
-            nc.sync.dma_start(out=raw[:], in_=w[:, c0:c1].rearrange("(p j) c -> p j c", j=PACK))
-            return raw
 
         def by_four(raw):
             return raw[:].rearrange("p j (m t) -> p m j t", t=PACK)
@@ -97,7 +91,7 @@ def tile_picked_maskdec_relu_p_kernel(tc, x_words, x_scales, w1, w2, w3, offs, m
         nc.sync.dma_start(out=w2_left[1][:], in_=w2_pairs[:, 0, :, HALF:])
         w2_right = sb("w2_right", [P, 2, H], F32)
         nc.sync.dma_start(out=w2_right[:], in_=w2_pairs[:, 1])
-        w1_left = load_rows("w1_left", w1, 0, EARLY)
+        nc.sync.dma_start(al_sb[:], al)
 
         def place(scales, picked):
             for r in range(PACK):
@@ -109,12 +103,14 @@ def tile_picked_maskdec_relu_p_kernel(tc, x_words, x_scales, w1, w2, w3, offs, m
         nc.vector.tensor_copy(out=q_picked[:], in_=xs[:].indirect(offs_sb[:]))
         nc.vector.tensor_copy(out=m_picked[:], in_=xs[:].indirect(mix_sb[:]))
         place(q_scales, q_picked)
-        w1_right = load_rows("w1_right", w1, EARLY, H)
-        nc.sync.dma_start(al_sb[:], al)
+        w1_raw = sb("w1_raw", [P, PACK, H], F32)
+        nc.sync.dma_start(out=w1_raw[:], in_=w1.rearrange("(p j) c -> p j c", j=PACK))
         w3_raw = shared.tile([P, PACK, N], F32, name="w3_raw", offset=8192, align_bytes=64)
         nc.sync.dma_start(out=w3_raw[:], in_=w3.rearrange("(p j) c -> p j c", j=PACK))
         place(m_scales, m_picked)
         nc.vector.tensor_copy(out=q_words[:], in_=xw[:].bitcast(U32).indirect(offs_sb[:]))
+        m_words = [sb("m_words0", [P, HALF], U32)]
+        nc.vector.tensor_copy(out=m_words[0][:], in_=xw[:].bitcast(U32).indirect(mix_sb[:, : HALF // LIST_ROWS]))
 
         def two_planes(raw, u):
             return by_four(raw)[:, :, :, 2 * u : 2 * u + 2]
@@ -137,34 +133,30 @@ def tile_picked_maskdec_relu_p_kernel(tc, x_words, x_scales, w1, w2, w3, offs, m
                 in_=w2_bf[u][:, PACK * lo : PACK * hi],
             )
 
-        m_words = sb("m_words", [P, S], U32, on="w2_bf0")
-        nc.vector.tensor_copy(out=m_words[:], in_=xw[:].bitcast(U32).indirect(mix_sb[:]))
+        m_words.append(sb("m_words1", [P, HALF], U32, on="w2_bf0"))
+        nc.vector.tensor_copy(out=m_words[1][:], in_=xw[:].bitcast(U32).indirect(mix_sb[:, HALF // LIST_ROWS :]))
         w1_bf = shared.tile([P, PACK * H], BF16, name="w1_bf", offset=16384, align_bytes=64)
-        nc.scalar.copy(out=dealt(w1_bf)[:, : EARLY // PACK], in_=by_four(w1_left))
-        first = []
-        for h, tag in enumerate(("s0", "e3")):
-            bank = psum.tile([P, HALF], F32, name="s_first%d" % h, tag=tag)
-            product(bank[:], w2_mx, 0, (q_words, q_scales), slice(h * HALF, (h + 1) * HALF))
-            first.append(bank)
-        s_banks = [None]
-        for t in range(1, PACK):
-            bank = psum.tile([P, S], F32, name="s_bank%d" % t, tag="s%d" % t)
-            product(bank[:], w2_mx, t, (q_words, q_scales), slice(0, S))
-            s_banks.append(bank)
-        nc.vector.tensor_copy(out=dealt(w1_bf)[:, EARLY // PACK :], in_=by_four(w1_right))
-        s_sb = [sb("s_sb%d" % t, [P, S], F32, on={3: "w1_right"}.get(t)) for t in range(PACK)]
-        for h in range(2):
-            nc.scalar.copy(out=s_sb[0][:, h * HALF : (h + 1) * HALF], in_=first[h][:])
-        for t in range(1, PACK - 1):
-            nc.scalar.copy(out=s_sb[t][:], in_=s_banks[t][:])
-        nc.vector.tensor_copy(out=s_sb[3][:], in_=s_banks[3][:])
+        halves = {}
+        for t in range(PACK - 1):
+            for h, tag in enumerate(("s%d" % t, "e%d" % (PACK - 1 - t))):
+                bank = psum.tile([P, HALF], F32, name="s_half%d_%d" % (t, h), tag=tag)
+                product(bank[:], w2_mx, t, (q_words, q_scales), slice(h * HALF, (h + 1) * HALF))
+                halves[t, h] = bank
+        s_last = psum.tile([P, S], F32, name="s_last", tag="s3")
+        product(s_last[:], w2_mx, PACK - 1, (q_words, q_scales), slice(0, S))
+        nc.vector.tensor_copy(out=dealt(w1_bf), in_=by_four(w1_raw))
+        s_sb = [sb("s_sb%d" % t, [P, S], F32, on={3: "w1_raw"}.get(t)) for t in range(PACK)]
+        for t in range(PACK - 1):
+            for h in range(2):
+                nc.scalar.copy(out=s_sb[t][:, h * HALF : (h + 1) * HALF], in_=halves[t, h][:])
+        nc.vector.tensor_copy(out=s_sb[3][:], in_=s_last[:])
         w1_mx = mx_tiles("w1", H)
         quantize(w1_mx, w1_bf, 0, H)
         e_banks = []
         for c in range(S // CHUNK):
             bank = psum.tile([P, PACK, CHUNK], F32, name="e_bank%d" % c, tag="e%d" % c)
             for t in range(PACK):
-                product(bank[:, t, :], w1_mx, t, (m_words, m_scales), slice(c * CHUNK, (c + 1) * CHUNK))
+                product(bank[:, t, :], w1_mx, t, (m_words[c // 2], m_scales[:, c // 2 * HALF :]), slice(c % 2 * CHUNK, (c % 2 + 1) * CHUNK))
             e_banks.append(bank)
 
         w3_mx = mx_tiles("w3", N)

@@ -103,14 +103,14 @@ def tile_picked_maskdec_relu_p_kernel(tc, x_words, x_scales, w1, w2, w3, offs, m
         nc.vector.tensor_copy(out=q_picked[:], in_=xs[:].indirect(offs_sb[:]))
         nc.vector.tensor_copy(out=m_picked[:], in_=xs[:].indirect(mix_sb[:]))
         place(q_scales, q_picked)
-        w1_raw = sb("w1_raw", [P, PACK, H], F32)
+        w1_raw = shared.tile([P, PACK, H], F32, name="w1_raw", offset=20480, align_bytes=64)
         nc.sync.dma_start(out=w1_raw[:], in_=w1.rearrange("(p j) c -> p j c", j=PACK))
         w3_raw = shared.tile([P, PACK, N], F32, name="w3_raw", offset=8192, align_bytes=64)
         nc.sync.dma_start(out=w3_raw[:], in_=w3.rearrange("(p j) c -> p j c", j=PACK))
         place(m_scales, m_picked)
         nc.vector.tensor_copy(out=q_words[:], in_=xw[:].bitcast(U32).indirect(offs_sb[:]))
-        m_words = [sb("m_words0", [P, HALF], U32)]
-        nc.vector.tensor_copy(out=m_words[0][:], in_=xw[:].bitcast(U32).indirect(mix_sb[:, : HALF // LIST_ROWS]))
+        m_words = [sb("m_words0", [P, CHUNK], U32)]
+        nc.vector.tensor_copy(out=m_words[0][:], in_=xw[:].bitcast(U32).indirect(mix_sb[:, : CHUNK // LIST_ROWS]))
 
         def two_planes(raw, u):
             return by_four(raw)[:, :, :, 2 * u : 2 * u + 2]
@@ -133,30 +133,45 @@ def tile_picked_maskdec_relu_p_kernel(tc, x_words, x_scales, w1, w2, w3, offs, m
                 in_=w2_bf[u][:, PACK * lo : PACK * hi],
             )
 
-        m_words.append(sb("m_words1", [P, HALF], U32, on="w2_bf0"))
-        nc.vector.tensor_copy(out=m_words[1][:], in_=xw[:].bitcast(U32).indirect(mix_sb[:, HALF // LIST_ROWS :]))
+        m_words.append(sb("m_words1", [P, S - CHUNK], U32, on="w2_bf0"))
+        nc.vector.tensor_copy(out=m_words[1][:], in_=xw[:].bitcast(U32).indirect(mix_sb[:, CHUNK // LIST_ROWS :]))
         w1_bf = shared.tile([P, PACK * H], BF16, name="w1_bf", offset=16384, align_bytes=64)
         halves = {}
-        for t in range(PACK - 1):
+        for t in range(PACK):
             for h, tag in enumerate(("s%d" % t, "e%d" % (PACK - 1 - t))):
                 bank = psum.tile([P, HALF], F32, name="s_half%d_%d" % (t, h), tag=tag)
                 product(bank[:], w2_mx, t, (q_words, q_scales), slice(h * HALF, (h + 1) * HALF))
                 halves[t, h] = bank
-        s_last = psum.tile([P, S], F32, name="s_last", tag="s3")
-        product(s_last[:], w2_mx, PACK - 1, (q_words, q_scales), slice(0, S))
-        nc.vector.tensor_copy(out=dealt(w1_bf), in_=by_four(w1_raw))
-        s_sb = [sb("s_sb%d" % t, [P, S], F32, on={3: "w1_raw"}.get(t)) for t in range(PACK)]
-        for t in range(PACK - 1):
+        s_sb = [sb("s_sb%d" % t, [P, S], F32) for t in range(2)]
+        s_sb += [shared.tile([P, S], F32, name="s_sb%d" % t, offset=20480 + 2048 * t, align_bytes=64) for t in (2, 3)]
+        mask_early = sb("mask_early", [P, PACK, 2 * CHUNK], F32)
+
+        def look_up(mask, t, first, width):
+            entries = al_sb[:, first // LIST_ROWS : (first + width) // LIST_ROWS]
+            nc.scalar.activation(mask[:, t, :], s_sb[t][:].indirect(entries), ACT.Sigmoid)
+
+        def empty(t, h, copy):
+            copy(out=s_sb[t][:, h * HALF : (h + 1) * HALF], in_=halves[t, h][:])
+
+        for t in range(2):
             for h in range(2):
-                nc.scalar.copy(out=s_sb[t][:, h * HALF : (h + 1) * HALF], in_=halves[t, h][:])
-        nc.vector.tensor_copy(out=s_sb[3][:], in_=s_last[:])
+                empty(t, h, nc.scalar.copy)
+        for t in range(2):
+            look_up(mask_early, t, 0, 2 * CHUNK)
+        nc.vector.tensor_copy(out=dealt(w1_bf), in_=by_four(w1_raw))
+        for t, h in ((2, 0), (2, 1), (3, 0)):
+            empty(t, h, nc.scalar.copy)
+        empty(3, 1, nc.vector.tensor_copy)
+        for t in range(2, PACK):
+            look_up(mask_early, t, 0, 2 * CHUNK)
         w1_mx = mx_tiles("w1", H)
         quantize(w1_mx, w1_bf, 0, H)
         e_banks = []
         for c in range(S // CHUNK):
             bank = psum.tile([P, PACK, CHUNK], F32, name="e_bank%d" % c, tag="e%d" % c)
             for t in range(PACK):
-                product(bank[:, t, :], w1_mx, t, (m_words[c // 2], m_scales[:, c // 2 * HALF :]), slice(c % 2 * CHUNK, (c % 2 + 1) * CHUNK))
+                words = m_words[0] if c == 0 else m_words[1][:, (c - 1) * CHUNK :]
+                product(bank[:, t, :], w1_mx, t, (words, m_scales[:, c * CHUNK :]), slice(0, CHUNK))
             e_banks.append(bank)
 
         w3_mx = mx_tiles("w3", N)
@@ -172,16 +187,10 @@ def tile_picked_maskdec_relu_p_kernel(tc, x_words, x_scales, w1, w2, w3, offs, m
                 in_=w3_bf[h][:],
             )
 
-        def look_up(mask, first, lo, width):
-            entries = al_sb[:, (first + lo) // LIST_ROWS : (first + lo + width) // LIST_ROWS]
-            for t in range(PACK):
-                nc.scalar.activation(mask[:, t, lo : lo + width], s_sb[t][:].indirect(entries), ACT.Sigmoid)
-
-        mask_early = sb("mask_early", [P, PACK, 2 * CHUNK], F32)
         mask_late = [shared.tile([P, PACK, CHUNK], F32, name="mask%d" % c, offset=16384 + c * 2048, align_bytes=64) for c in range(2)]
-        look_up(mask_early, 0, 0, 2 * CHUNK)
-        look_up(mask_late[0], 2 * CHUNK, 0, CHUNK)
-        look_up(mask_late[1], 3 * CHUNK, 0, CHUNK)
+        for c in range(2):
+            for t in range(PACK):
+                look_up(mask_late[c], t, (2 + c) * CHUNK, CHUNK)
 
         z_bf = shared.tile([P, PACK * 2 * CHUNK], BF16, name="z_bf", offset=2048, align_bytes=64)
         z_mx = [mx_tiles("z%d" % c, CHUNK) for c in range(S // CHUNK)]

@@ -82,13 +82,13 @@ def tile_picked_maskdec_relu_p_kernel(tc, x_words, x_scales, w1, w2, w3, offs, m
         nc.scalar.activation(warm_out[:], warm_in[:], ACT.Sigmoid)
 
         w2_pairs = w2.rearrange("(p u j) c -> p u j c", u=2, j=2)
-        w2_left = [sb("w2_left%d" % h, [P, 2, HALF], F32) for h in range(2)]
-        nc.sync.dma_start(out=w2_left[0][:], in_=w2_pairs[:, 0, :, :HALF])
+        w2_left = [sb("w2_left%d" % j, [P, 1, H], F32) for j in range(2)]
+        nc.sync.dma_start(out=w2_left[0][:], in_=w2_pairs[:, 0, 0:1])
         nc.sync.dma_start(offs_sb[:], offs)
         nc.sync.dma_start(mix_sb[:], mix)
         nc.sync.dma_start(out=xs[0:P:BLOCK, :].bitcast(I32), in_=x_scales[0].bitcast(I32))
         nc.sync.dma_start(out=xw[:], in_=x_words[0].rearrange("p c r -> p (c r)").bitcast(I32))
-        nc.sync.dma_start(out=w2_left[1][:], in_=w2_pairs[:, 0, :, HALF:])
+        nc.sync.dma_start(out=w2_left[1][:], in_=w2_pairs[:, 0, 1:2])
         w2_right = sb("w2_right", [P, 2, H], F32)
         nc.sync.dma_start(out=w2_right[:], in_=w2_pairs[:, 1])
         nc.sync.dma_start(al_sb[:], al)
@@ -118,29 +118,36 @@ def tile_picked_maskdec_relu_p_kernel(tc, x_words, x_scales, w1, w2, w3, offs, m
         def dealt_pair(grouped):
             return grouped[:].rearrange("p (t m j) -> p m j t", t=2, j=PACK)
 
-        w2_bf = [sb("w2_bf%d" % u, [P, PACK * HALF], BF16) for u in range(2)]
-        for h in range(2):
-            for u in range(2):
-                nc.scalar.copy(out=dealt_pair(w2_bf[u])[:, h * GROUPS : (h + 1) * GROUPS, 0:2], in_=two_planes(w2_left[h], u))
-        for t in range(2):
-            nc.vector.tensor_copy(out=dealt_pair(w2_bf[0])[:, :, 2:4, t], in_=by_four(w2_right)[:, :, :, t])
-        nc.scalar.copy(out=dealt_pair(w2_bf[1])[:, :, 2:4], in_=two_planes(w2_right, 1))
-        w2_mx = mx_tiles("w2", H)
-        for u, lo, hi in ((0, 0, P), (0, P, HALF), (1, 0, HALF)):
-            nc.vector.quantize_mx(
-                out=w2_mx[0][:, u * HALF + lo : u * HALF + hi].bitcast(FP8X4),
-                scales=w2_mx[1][:, u * HALF + lo : u * HALF + hi],
-                in_=w2_bf[u][:, PACK * lo : PACK * hi],
-            )
+        def one_plane(grouped):
+            return grouped[:].rearrange("p (m j) -> p m j", j=PACK)
 
-        m_words.append(sb("m_words1", [P, S - CHUNK], U32, on="w2_bf0"))
+        w2_plane = [shared.tile([P, PACK * P], BF16, name="w2_plane0", offset=29696, align_bytes=64), sb("w2_plane1", [P, PACK * P], BF16)]
+        w2_pair = sb("w2_pair", [P, PACK * HALF], BF16)
+        for j in range(2):
+            for t in range(2):
+                nc.scalar.copy(out=one_plane(w2_plane[t])[:, :, j : j + 1], in_=by_four(w2_left[j])[:, :, :, t])
+            nc.scalar.copy(out=dealt_pair(w2_pair)[:, :, j : j + 1], in_=two_planes(w2_left[j], 1))
+        for t in range(2):
+            nc.vector.tensor_copy(out=one_plane(w2_plane[t])[:, :, 2:4], in_=by_four(w2_right)[:, :, :, t])
+        nc.scalar.copy(out=dealt_pair(w2_pair)[:, :, 2:4], in_=two_planes(w2_right, 1))
+        w2_mx = [mx_tiles("w2_first", HALF)]
+        for t in range(2):
+            nc.vector.quantize_mx(
+                out=w2_mx[0][0][:, t * P : (t + 1) * P].bitcast(FP8X4),
+                scales=w2_mx[0][1][:, t * P : (t + 1) * P],
+                in_=w2_plane[t][:],
+            )
+        m_words.append(shared.tile([P, S - CHUNK], U32, name="m_words1", offset=28672, align_bytes=64))
         nc.vector.tensor_copy(out=m_words[1][:], in_=xw[:].bitcast(U32).indirect(mix_sb[:, CHUNK // LIST_ROWS :]))
+        late_codes = shared.tile([P, HALF], U32, name="w2_late_codes", offset=30208, align_bytes=64)
+        w2_mx.append((late_codes, sb("w2_late_scales", [P, HALF], U8)))
+        quantize(w2_mx[1], w2_pair, 0, HALF)
         w1_bf = shared.tile([P, PACK * H], BF16, name="w1_bf", offset=16384, align_bytes=64)
         halves = {}
         for t in range(PACK):
             for h, tag in enumerate(("s%d" % t, "e%d" % (PACK - 1 - t))):
                 bank = psum.tile([P, HALF], F32, name="s_half%d_%d" % (t, h), tag=tag)
-                product(bank[:], w2_mx, t, (q_words, q_scales), slice(h * HALF, (h + 1) * HALF))
+                product(bank[:], w2_mx[t // 2], t % 2, (q_words, q_scales), slice(h * HALF, (h + 1) * HALF))
                 halves[t, h] = bank
         s_sb = [sb("s_sb%d" % t, [P, S], F32) for t in range(2)]
         s_sb += [shared.tile([P, S], F32, name="s_sb%d" % t, offset=20480 + 2048 * t, align_bytes=64) for t in (2, 3)]
@@ -159,9 +166,9 @@ def tile_picked_maskdec_relu_p_kernel(tc, x_words, x_scales, w1, w2, w3, offs, m
         for t in range(2):
             look_up(mask_early, t, 0, 2 * CHUNK)
         nc.vector.tensor_copy(out=dealt(w1_bf), in_=by_four(w1_raw))
-        for t, h in ((2, 0), (2, 1), (3, 0)):
-            empty(t, h, nc.scalar.copy)
-        empty(3, 1, nc.vector.tensor_copy)
+        for h in range(2):
+            empty(2, h, nc.scalar.copy)
+            empty(3, h, nc.vector.tensor_copy)
         for t in range(2, PACK):
             look_up(mask_early, t, 0, 2 * CHUNK)
         w1_mx = mx_tiles("w1", H)
@@ -174,18 +181,33 @@ def tile_picked_maskdec_relu_p_kernel(tc, x_words, x_scales, w1, w2, w3, offs, m
                 product(bank[:, t, :], w1_mx, t, (words, m_scales[:, c * CHUNK :]), slice(0, CHUNK))
             e_banks.append(bank)
 
-        w3_mx = mx_tiles("w3", N)
-        w3_bf = []
-        for h in range(2):
-            half = shared.tile([P, PACK * HALF], BF16, name="w3_bf%d" % h, offset=2048 + 2048 * h, align_bytes=64)
-            nc.vector.tensor_copy(out=in_order(half), in_=by_four(w3_raw)[:, h * GROUPS : (h + 1) * GROUPS])
-            w3_bf.append(half)
-        for h in range(2):
+        w3_mx = mx_tiles("w3", N - P)
+        w3_last = (sb("w3_last_codes", [P, P], U32, on="mask_early"), sb("w3_last_scales", [P, P], U8))
+        w3_cuts = (0, HALF, N - P, N)
+        w3_bf = [
+            shared.tile([P, PACK * (w3_cuts[i + 1] - w3_cuts[i])], BF16, name="w3_bf%d" % i, offset=2048 + 2048 * min(i, 1), align_bytes=64)
+            for i in range(3)
+        ]
+
+        def quantize_w3(i):
             nc.vector.quantize_mx(
-                out=w3_mx[0][:, h * HALF : (h + 1) * HALF].bitcast(FP8X4),
-                scales=w3_mx[1][:, h * HALF : (h + 1) * HALF],
-                in_=w3_bf[h][:],
+                out=w3_mx[0][:, w3_cuts[i] : w3_cuts[i + 1]].bitcast(FP8X4),
+                scales=w3_mx[1][:, w3_cuts[i] : w3_cuts[i + 1]],
+                in_=w3_bf[i][:],
             )
+
+        for i in range(2):
+            nc.vector.tensor_copy(out=in_order(w3_bf[i]), in_=by_four(w3_raw)[:, w3_cuts[i] // PACK : w3_cuts[i + 1] // PACK])
+        for i in range(2):
+            quantize_w3(i)
+        nc.gpsimd.tensor_scalar(
+            out=w3_bf[2][:].rearrange("p (c j) -> p c j", j=PACK),
+            in0=w3_raw[:, :, w3_cuts[2] :].rearrange("p j c -> p c j"),
+            scalar1=1.0,
+            scalar2=0.0,
+            op0=ALU.mult,
+            op1=ALU.add,
+        )
 
         mask_late = [shared.tile([P, PACK, CHUNK], F32, name="mask%d" % c, offset=16384 + c * 2048, align_bytes=64) for c in range(2)]
         for c in range(2):
@@ -214,7 +236,8 @@ def tile_picked_maskdec_relu_p_kernel(tc, x_words, x_scales, w1, w2, w3, offs, m
         def decode(c, m0, count, tag):
             bank = psum.tile([P, count, CHUNK], F32, name="o_bank%d_%d" % (c, m0), tag=tag)
             for m in range(count):
-                product(bank[:, m, :], w3_mx, m0 + m, z_mx[c], slice(0, CHUNK))
+                weights, block = (w3_last, 0) if m0 + m == PACK - 1 else (w3_mx, m0 + m)
+                product(bank[:, m, :], weights, block, z_mx[c], slice(0, CHUNK))
             return bank
 
         def leave(c, m0, count, bank, copy):
@@ -225,6 +248,7 @@ def tile_picked_maskdec_relu_p_kernel(tc, x_words, x_scales, w1, w2, w3, offs, m
         masked(0, z_of(0))
         masked(1, z_of(1))
         quantize(z_mx[0], z_of(0), 0, CHUNK)
+        quantize(w3_last, w3_bf[2], 0, P)
         quantize(z_mx[1], z_of(1), 0, CHUNK)
         bank0 = [decode(0, 0, 2, "s0"), decode(0, 2, 2, "s3")]
         bank1 = decode(1, 0, PACK, "s1")

@@ -82,13 +82,13 @@ def tile_picked_maskdec_relu_p_kernel(tc, x_words, x_scales, w1, w2, w3, offs, m
         nc.scalar.activation(warm_out[:], warm_in[:], ACT.Sigmoid)
 
         w2_pairs = w2.rearrange("(p u j) c -> p u j c", u=2, j=2)
-        w2_left = [sb("w2_left%d" % j, [P, 1, H], F32) for j in range(2)]
-        nc.sync.dma_start(out=w2_left[0][:], in_=w2_pairs[:, 0, 0:1])
+        w2_left = [sb("w2_left%d" % h, [P, 2, HALF], F32) for h in range(2)]
+        nc.sync.dma_start(out=w2_left[0][:], in_=w2_pairs[:, 0, :, :HALF])
         nc.sync.dma_start(offs_sb[:], offs)
         nc.sync.dma_start(mix_sb[:], mix)
         nc.sync.dma_start(out=xs[0:P:BLOCK, :].bitcast(I32), in_=x_scales[0].bitcast(I32))
         nc.sync.dma_start(out=xw[:], in_=x_words[0].rearrange("p c r -> p (c r)").bitcast(I32))
-        nc.sync.dma_start(out=w2_left[1][:], in_=w2_pairs[:, 0, 1:2])
+        nc.sync.dma_start(out=w2_left[1][:], in_=w2_pairs[:, 0, :, HALF:])
         w2_right = sb("w2_right", [P, 2, H], F32)
         nc.sync.dma_start(out=w2_right[:], in_=w2_pairs[:, 1])
         nc.sync.dma_start(al_sb[:], al)
@@ -123,19 +123,22 @@ def tile_picked_maskdec_relu_p_kernel(tc, x_words, x_scales, w1, w2, w3, offs, m
 
         w2_plane = [shared.tile([P, PACK * P], BF16, name="w2_plane0", offset=29696, align_bytes=64), sb("w2_plane1", [P, PACK * P], BF16)]
         w2_pair = sb("w2_pair", [P, PACK * HALF], BF16)
-        for j in range(2):
+        for h in range(2):
+            groups = slice(h * GROUPS, (h + 1) * GROUPS)
             for t in range(2):
-                nc.scalar.copy(out=one_plane(w2_plane[t])[:, :, j : j + 1], in_=by_four(w2_left[j])[:, :, :, t])
-            nc.scalar.copy(out=dealt_pair(w2_pair)[:, :, j : j + 1], in_=two_planes(w2_left[j], 1))
-        for t in range(2):
-            nc.vector.tensor_copy(out=one_plane(w2_plane[t])[:, :, 2:4], in_=by_four(w2_right)[:, :, :, t])
+                nc.scalar.copy(out=one_plane(w2_plane[t])[:, groups, 0:2], in_=by_four(w2_left[h])[:, :, :, t])
+            nc.scalar.copy(out=dealt_pair(w2_pair)[:, groups, 0:2], in_=two_planes(w2_left[h], 1))
+        for h in range(2):
+            groups = slice(h * GROUPS, (h + 1) * GROUPS)
+            nc.vector.tensor_copy(out=one_plane(w2_plane[0])[:, groups, 2:4], in_=by_four(w2_right)[:, groups, :, 0])
+        nc.scalar.copy(out=one_plane(w2_plane[1])[:, :, 2:4], in_=by_four(w2_right)[:, :, :, 1])
         nc.scalar.copy(out=dealt_pair(w2_pair)[:, :, 2:4], in_=two_planes(w2_right, 1))
         w2_mx = [mx_tiles("w2_first", HALF)]
-        for t in range(2):
+        for t, lo, hi in ((0, 0, GROUPS), (0, GROUPS, P), (1, 0, P)):
             nc.vector.quantize_mx(
-                out=w2_mx[0][0][:, t * P : (t + 1) * P].bitcast(FP8X4),
-                scales=w2_mx[0][1][:, t * P : (t + 1) * P],
-                in_=w2_plane[t][:],
+                out=w2_mx[0][0][:, t * P + lo : t * P + hi].bitcast(FP8X4),
+                scales=w2_mx[0][1][:, t * P + lo : t * P + hi],
+                in_=w2_plane[t][:, PACK * lo : PACK * hi],
             )
         m_words.append(shared.tile([P, S - CHUNK], U32, name="m_words1", offset=28672, align_bytes=64))
         nc.vector.tensor_copy(out=m_words[1][:], in_=xw[:].bitcast(U32).indirect(mix_sb[:, CHUNK // LIST_ROWS :]))
@@ -144,13 +147,15 @@ def tile_picked_maskdec_relu_p_kernel(tc, x_words, x_scales, w1, w2, w3, offs, m
         quantize(w2_mx[1], w2_pair, 0, HALF)
         w1_bf = shared.tile([P, PACK * H], BF16, name="w1_bf", offset=16384, align_bytes=64)
         halves = {}
-        for t in range(PACK):
+        for t in range(PACK - 1):
             for h, tag in enumerate(("s%d" % t, "e%d" % (PACK - 1 - t))):
                 bank = psum.tile([P, HALF], F32, name="s_half%d_%d" % (t, h), tag=tag)
                 product(bank[:], w2_mx[t // 2], t % 2, (q_words, q_scales), slice(h * HALF, (h + 1) * HALF))
                 halves[t, h] = bank
-        s_sb = [sb("s_sb%d" % t, [P, S], F32) for t in range(2)]
-        s_sb += [shared.tile([P, S], F32, name="s_sb%d" % t, offset=20480 + 2048 * t, align_bytes=64) for t in (2, 3)]
+        s_last = psum.tile([P, S], F32, name="s_last", tag="s3")
+        product(s_last[:], w2_mx[1], 1, (q_words, q_scales), slice(0, S))
+        s_sb = [sb("s_sb%d" % t, [P, S], F32) for t in range(PACK - 1)]
+        s_sb.append(shared.tile([P, S], F32, name="s_sb3", offset=20480, align_bytes=64))
         mask_early = sb("mask_early", [P, PACK, 2 * CHUNK], F32)
 
         def look_up(mask, t, first, width):
@@ -160,16 +165,14 @@ def tile_picked_maskdec_relu_p_kernel(tc, x_words, x_scales, w1, w2, w3, offs, m
         def empty(t, h, copy):
             copy(out=s_sb[t][:, h * HALF : (h + 1) * HALF], in_=halves[t, h][:])
 
-        for t in range(2):
+        for t in range(PACK - 1):
             for h in range(2):
                 empty(t, h, nc.scalar.copy)
-        for t in range(2):
-            look_up(mask_early, t, 0, 2 * CHUNK)
+            if t > 0:
+                look_up(mask_early, t - 1, 0, 2 * CHUNK)
         nc.vector.tensor_copy(out=dealt(w1_bf), in_=by_four(w1_raw))
-        for h in range(2):
-            empty(2, h, nc.scalar.copy)
-            empty(3, h, nc.vector.tensor_copy)
-        for t in range(2, PACK):
+        nc.vector.tensor_copy(out=s_sb[3][:], in_=s_last[:])
+        for t in (2, 3):
             look_up(mask_early, t, 0, 2 * CHUNK)
         w1_mx = mx_tiles("w1", H)
         quantize(w1_mx, w1_bf, 0, H)

@@ -188,7 +188,7 @@ def tile_picked_maskdec_relu_p_kernel(tc, x_words, x_scales, w1, w2, w3, offs, m
         w3_last = (sb("w3_last_codes", [P, P], U32, on="mask_early"), sb("w3_last_scales", [P, P], U8))
         w3_cuts = (0, HALF, N - P, N)
         w3_bf = [
-            shared.tile([P, PACK * (w3_cuts[i + 1] - w3_cuts[i])], BF16, name="w3_bf%d" % i, offset=2048 + 2048 * min(i, 1), align_bytes=64)
+            shared.tile([P, PACK * (w3_cuts[i + 1] - w3_cuts[i])], BF16, name="w3_bf%d" % i, offset=(2048, 6144, 4032)[i], align_bytes=64)
             for i in range(3)
         ]
 
@@ -217,7 +217,7 @@ def tile_picked_maskdec_relu_p_kernel(tc, x_words, x_scales, w1, w2, w3, offs, m
             for t in range(PACK):
                 look_up(mask_late[c], t, (2 + c) * CHUNK, CHUNK)
 
-        z_bf = shared.tile([P, PACK * 2 * CHUNK], BF16, name="z_bf", offset=2048, align_bytes=64)
+        z_bf = shared.tile([P, PACK * 2 * CHUNK], BF16, name="z_bf", offset=1984, align_bytes=64)
         z_mx = [mx_tiles("z%d" % c, CHUNK) for c in range(S // CHUNK)]
         out_rows = out.rearrange("(m p) j -> p m j", p=P)
 
@@ -259,7 +259,7 @@ def tile_picked_maskdec_relu_p_kernel(tc, x_words, x_scales, w1, w2, w3, offs, m
         leave(0, 0, 2, bank0[0], nc.vector.tensor_copy)
         quantize(z_mx[2], z_of(2), 0, CHUNK)
         bank2 = decode(2, 0, PACK, "s2")
-        z_last = sb("z_last", [P, PACK * CHUNK], BF16, on="z1_codes")
+        z_last = sb("z_last", [P, PACK * CHUNK], BF16, on="z0_codes")
         masked(3, z_last[:])
         quantize(z_mx[3], z_last, 0, CHUNK)
         leave(0, 2, 2, bank0[1], nc.scalar.copy)

@@ -236,34 +236,36 @@ def tile_picked_maskdec_relu_p_kernel(tc, x_words, x_scales, w1, w2, w3, offs, m
         def z_of(c):
             return z_bf[:, c % 2 * PACK * CHUNK : (c % 2 + 1) * PACK * CHUNK]
 
-        def decode(c, m0, count, tag):
-            bank = psum.tile([P, count, CHUNK], F32, name="o_bank%d_%d" % (c, m0), tag=tag)
-            for m in range(count):
-                weights, block = (w3_last, 0) if m0 + m == PACK - 1 else (w3_mx, m0 + m)
-                product(bank[:, m, :], weights, block, z_mx[c], slice(0, CHUNK))
+        def decode(chunks, m0, count, tag):
+            bank = psum.tile([P, count, len(chunks) * CHUNK], F32, name="o_bank%d_%d" % (chunks[0], m0), tag=tag)
+            for i, c in enumerate(chunks):
+                for m in range(count):
+                    weights, block = (w3_last, 0) if m0 + m == PACK - 1 else (w3_mx, m0 + m)
+                    product(bank[:, m, i * CHUNK : (i + 1) * CHUNK], weights, block, z_mx[c], slice(0, CHUNK))
             return bank
 
-        def leave(c, m0, count, bank, copy):
-            res = sb("res%d_%d" % (c, m0), [P, count, CHUNK], F32)
+        def leave(c, m0, count, bank, copy, width=CHUNK):
+            res = sb("res%d_%d" % (c, m0), [P, count, width], F32)
             copy(out=res[:], in_=bank[:])
-            nc.sync.dma_start(out=out_rows[:, m0 : m0 + count, c * CHUNK : (c + 1) * CHUNK], in_=res[:])
+            nc.sync.dma_start(out=out_rows[:, m0 : m0 + count, c * CHUNK : c * CHUNK + width], in_=res[:])
 
         masked(0, z_of(0))
         masked(1, z_of(1))
         quantize(z_mx[0], z_of(0), 0, CHUNK)
-        quantize(w3_last, w3_bf[2], 0, P)
         quantize(z_mx[1], z_of(1), 0, CHUNK)
-        bank0 = [decode(0, 0, 2, "s0"), decode(0, 2, 2, "s3")]
-        bank1 = decode(1, 0, PACK, "s1")
+        quantize(w3_last, w3_bf[2], 0, P)
+        bank0 = decode([0], 0, 2, "s0")
+        bank1 = decode([1], 0, 2, "s3")
+        bank01 = decode([0, 1], 2, 2, "s1")
         masked(2, z_of(2))
-        leave(0, 0, 2, bank0[0], nc.vector.tensor_copy)
+        leave(0, 0, 2, bank0, nc.vector.tensor_copy)
         quantize(z_mx[2], z_of(2), 0, CHUNK)
-        bank2 = decode(2, 0, PACK, "s2")
+        bank2 = decode([2], 0, PACK, "s2")
         z_last = sb("z_last", [P, PACK * CHUNK], BF16, on="z0_codes")
         masked(3, z_last[:])
         quantize(z_mx[3], z_last, 0, CHUNK)
-        leave(0, 2, 2, bank0[1], nc.scalar.copy)
-        leave(1, 0, PACK, bank1, nc.scalar.copy)
+        leave(1, 0, 2, bank1, nc.scalar.copy)
+        leave(0, 2, 2, bank01, nc.scalar.copy, 2 * CHUNK)
         leave(2, 0, PACK, bank2, nc.scalar.copy)
-        leave(3, 0, 2, decode(3, 0, 2, "e1"), nc.scalar.copy)
-        leave(3, 2, 2, decode(3, 2, 2, "e0"), nc.vector.tensor_copy)
+        leave(3, 0, 2, decode([3], 0, 2, "e1"), nc.scalar.copy)
+        leave(3, 2, 2, decode([3], 2, 2, "e0"), nc.vector.tensor_copy)

@@ -91,7 +91,6 @@ def tile_picked_maskdec_relu_p_kernel(tc, x_words, x_scales, w1, w2, w3, offs, m
         nc.sync.dma_start(out=w2_left[1][:], in_=w2_pairs[:, 0, :, HALF:])
         w2_right = sb("w2_right", [P, 2, H], F32)
         nc.sync.dma_start(out=w2_right[:], in_=w2_pairs[:, 1])
-        nc.sync.dma_start(al_sb[:], al)
 
         def place(scales, picked):
             for r in range(PACK):
@@ -105,6 +104,7 @@ def tile_picked_maskdec_relu_p_kernel(tc, x_words, x_scales, w1, w2, w3, offs, m
         place(q_scales, q_picked)
         w1_raw = shared.tile([P, PACK, H], F32, name="w1_raw", offset=20480, align_bytes=64)
         nc.sync.dma_start(out=w1_raw[:], in_=w1.rearrange("(p j) c -> p j c", j=PACK))
+        nc.sync.dma_start(al_sb[:], al)
         w3_raw = shared.tile([P, PACK, N], F32, name="w3_raw", offset=8192, align_bytes=64)
         nc.sync.dma_start(out=w3_raw[:], in_=w3.rearrange("(p j) c -> p j c", j=PACK))
         place(m_scales, m_picked)
@@ -121,25 +121,23 @@ def tile_picked_maskdec_relu_p_kernel(tc, x_words, x_scales, w1, w2, w3, offs, m
         def one_plane(grouped):
             return grouped[:].rearrange("p (m j) -> p m j", j=PACK)
 
-        w2_plane = [shared.tile([P, PACK * P], BF16, name="w2_plane0", offset=29696, align_bytes=64), sb("w2_plane1", [P, PACK * P], BF16)]
+        w2_low = [sb("w2_low%d" % t, [P, PACK * GROUPS], BF16) for t in range(2)]
+        w2_high = shared.tile([P, PACK * P], BF16, name="w2_high", offset=29696, align_bytes=64)
         w2_pair = sb("w2_pair", [P, PACK * HALF], BF16)
-        for h in range(2):
-            groups = slice(h * GROUPS, (h + 1) * GROUPS)
-            for t in range(2):
-                nc.scalar.copy(out=one_plane(w2_plane[t])[:, groups, 0:2], in_=by_four(w2_left[h])[:, :, :, t])
-            nc.scalar.copy(out=dealt_pair(w2_pair)[:, groups, 0:2], in_=two_planes(w2_left[h], 1))
-        for h in range(2):
-            groups = slice(h * GROUPS, (h + 1) * GROUPS)
-            nc.vector.tensor_copy(out=one_plane(w2_plane[0])[:, groups, 2:4], in_=by_four(w2_right)[:, groups, :, 0])
-        nc.scalar.copy(out=one_plane(w2_plane[1])[:, :, 2:4], in_=by_four(w2_right)[:, :, :, 1])
+        for t in range(2):
+            nc.scalar.copy(out=one_plane(w2_low[t])[:, :, 0:2], in_=by_four(w2_left[0])[:, :, :, t])
+        nc.scalar.copy(out=dealt_pair(w2_pair)[:, :GROUPS, 0:2], in_=two_planes(w2_left[0], 1))
+        nc.scalar.copy(out=dealt_pair(w2_high)[:, :, 0:2], in_=two_planes(w2_left[1], 0))
+        nc.scalar.copy(out=dealt_pair(w2_pair)[:, GROUPS:, 0:2], in_=two_planes(w2_left[1], 1))
+        nc.vector.tensor_copy(out=dealt_pair(w2_high)[:, :, 2:4], in_=two_planes(w2_right, 0)[:, GROUPS:])
+        for t in range(2):
+            nc.scalar.copy(out=one_plane(w2_low[t])[:, :, 2:4], in_=by_four(w2_right)[:, :GROUPS, :, t])
         nc.scalar.copy(out=dealt_pair(w2_pair)[:, :, 2:4], in_=two_planes(w2_right, 1))
         w2_mx = [mx_tiles("w2_first", HALF)]
-        for t, lo, hi in ((0, 0, GROUPS), (0, GROUPS, P), (1, 0, P)):
-            nc.vector.quantize_mx(
-                out=w2_mx[0][0][:, t * P + lo : t * P + hi].bitcast(FP8X4),
-                scales=w2_mx[0][1][:, t * P + lo : t * P + hi],
-                in_=w2_plane[t][:, PACK * lo : PACK * hi],
-            )
+        for t, h in ((0, 0), (0, 1), (1, 1), (1, 0)):
+            cols = slice(t * P + h * GROUPS, t * P + (h + 1) * GROUPS)
+            grouped = w2_high[:, t * HALF : (t + 1) * HALF] if h else w2_low[t][:]
+            nc.vector.quantize_mx(out=w2_mx[0][0][:, cols].bitcast(FP8X4), scales=w2_mx[0][1][:, cols], in_=grouped)
         m_words.append(shared.tile([P, S - CHUNK], U32, name="m_words1", offset=28672, align_bytes=64))
         nc.vector.tensor_copy(out=m_words[1][:], in_=xw[:].bitcast(U32).indirect(mix_sb[:, CHUNK // LIST_ROWS :]))
         late_codes = shared.tile([P, HALF], U32, name="w2_late_codes", offset=30208, align_bytes=64)
@@ -154,8 +152,8 @@ def tile_picked_maskdec_relu_p_kernel(tc, x_words, x_scales, w1, w2, w3, offs, m
                 halves[t, h] = bank
         s_last = psum.tile([P, S], F32, name="s_last", tag="s3")
         product(s_last[:], w2_mx[1], 1, (q_words, q_scales), slice(0, S))
-        s_sb = [sb("s_sb%d" % t, [P, S], F32) for t in range(PACK - 1)]
-        s_sb.append(shared.tile([P, S], F32, name="s_sb3", offset=20480, align_bytes=64))
+        s_sb = [sb("s_sb%d" % t, [P, S], F32) for t in range(2)]
+        s_sb.extend(shared.tile([P, S], F32, name="s_sb%d" % t, offset=16384 + 2048 * t, align_bytes=64) for t in (2, 3))
         mask_early = sb("mask_early", [P, PACK, 2 * CHUNK], F32)
 
         def look_up(mask, t, first, width):
@@ -165,14 +163,16 @@ def tile_picked_maskdec_relu_p_kernel(tc, x_words, x_scales, w1, w2, w3, offs, m
         def empty(t, h, copy):
             copy(out=s_sb[t][:, h * HALF : (h + 1) * HALF], in_=halves[t, h][:])
 
-        for t in range(PACK - 1):
+        for t in range(2):
             for h in range(2):
                 empty(t, h, nc.scalar.copy)
-            if t > 0:
-                look_up(mask_early, t - 1, 0, 2 * CHUNK)
+        for t in range(2):
+            look_up(mask_early, t, 0, 2 * CHUNK)
         nc.vector.tensor_copy(out=dealt(w1_bf), in_=by_four(w1_raw))
         nc.vector.tensor_copy(out=s_sb[3][:], in_=s_last[:])
-        for t in (2, 3):
+        for h in range(2):
+            empty(2, h, nc.scalar.copy)
+        for t in (3, 2):
             look_up(mask_early, t, 0, 2 * CHUNK)
         w1_mx = mx_tiles("w1", H)
         quantize(w1_mx, w1_bf, 0, H)

from contextlib import ExitStack

import concourse.mybir as mybir

K, T, S, H, N = 512, 2048, 512, 512, 512
FLOPS = 2 * K * H * S * 2 + 2 * H * N * S

F32 = mybir.dt.float32
BF16 = mybir.dt.bfloat16
I32 = mybir.dt.int32
U32 = mybir.dt.uint32
U16 = mybir.dt.uint16
U8 = mybir.dt.uint8
FP8X4 = mybir.dt.float8_e4m3fn_x4
ALU = mybir.AluOpType
ACT = mybir.ActivationFunctionType

P = 128
PACK = 4
LIST_ROWS = 16
QUADRANT = 32
BLOCK = 8
HALF = H // 2
CHUNK = 128
GROUPS = HALF // PACK


def tile_picked_maskdec_relu_p_kernel(tc, x_words, x_scales, w1, w2, w3, offs, mix, al, out):
    nc = tc.nc
    with ExitStack() as ctx:
        keep = ctx.enter_context(tc.tile_pool(name="keep", bufs=1))
        psum = ctx.enter_context(tc.psum_pool(name="psum", bufs=1))

        def sb(name, shape, dtype, on=None):
            return keep.tile(shape, dtype, name=name, tag=on or name, align_bytes=64)

        def by_four(raw):
            return raw[:].rearrange("p j (m t) -> p m j t", t=PACK)

        def dealt(grouped):
            return grouped[:].rearrange("p (t m j) -> p m j t", t=PACK, j=PACK)

        def in_order(grouped):
            return grouped[:].rearrange("p (m t j) -> p m j t", t=PACK, j=PACK)

        def mx_tiles(name, width):
            return sb(name + "_codes", [P, width], U32), sb(name + "_scales", [P, width], U8)

        def quantize(mx, grouped, c0, c1):
            nc.vector.quantize_mx(
                out=mx[0][:, c0:c1].bitcast(FP8X4),
                scales=mx[1][:, c0:c1],
                in_=grouped[:, PACK * c0 : PACK * c1],
            )

        def product(dst, weights, m, moving, cols):
            nc.tensor.matmul_mx(
                out=dst,
                lhsT=weights[0][:, m * P : (m + 1) * P].bitcast(FP8X4),
                lhsT_scale=weights[1][:, m * P : (m + 1) * P],
                rhs=moving[0][:, cols].bitcast(FP8X4),
                rhs_scale=moving[1][:, cols],
                start=True,
                stop=True,
            )

        shared = ctx.enter_context(tc.tile_pool(name="shared", bufs=1))
        offs_sb = sb("offs_sb", [P, S // LIST_ROWS], U16)
        mix_sb = sb("mix_sb", [P, S // LIST_ROWS], U16)
        al_sb = sb("al_sb", [P, S // LIST_ROWS], U16)
        xw = sb("xw", [P, T], I32)
        xs = sb("xs", [P, T], U8)
        warm_in = sb("warm_in", [P, 8], F32)
        warm_out = sb("warm_out", [P, 8], F32)

        nc.vector.memset(xs[:].bitcast(I32), 0)
        q_scales = sb("q_scales", [P, S], U8)
        m_scales = sb("m_scales", [P, S], U8)
        nc.vector.memset(warm_in[:], 0.0)
        nc.vector.memset(q_scales[:].bitcast(I32), 0)
        nc.vector.memset(m_scales[:].bitcast(I32), 0)
        nc.scalar.activation(warm_out[:], warm_in[:], ACT.Sigmoid)

        w2_pairs = w2.rearrange("(p u j) c -> p u j c", u=2, j=2)
        w2_left = [sb("w2_left%d" % h, [P, 2, HALF], F32) for h in range(2)]
        nc.sync.dma_start(out=w2_left[0][:], in_=w2_pairs[:, 0, :, :HALF])
        nc.sync.dma_start(offs_sb[:], offs)
        nc.sync.dma_start(mix_sb[:], mix)
        nc.sync.dma_start(out=xs[0:P:BLOCK, :].bitcast(I32), in_=x_scales[0].bitcast(I32))
        nc.sync.dma_start(out=xw[:], in_=x_words[0].rearrange("p c r -> p (c r)").bitcast(I32))
        nc.sync.dma_start(out=w2_left[1][:], in_=w2_pairs[:, 0, :, HALF:])
        w2_right = sb("w2_right", [P, 2, H], F32)
        nc.sync.dma_start(out=w2_right[:], in_=w2_pairs[:, 1])

        def place(scales, picked):
            for r in range(PACK):
                nc.sync.dma_start(out=scales[r:P:QUADRANT, :].bitcast(I32), in_=picked[BLOCK * r : P : QUADRANT, :].bitcast(I32))

        q_words = sb("q_words", [P, S], U32)
        q_picked = sb("q_picked", [P, S], U8)
        m_picked = sb("m_picked", [P, S], U8)
        nc.vector.tensor_copy(out=q_picked[:], in_=xs[:].indirect(offs_sb[:]))
        nc.vector.tensor_copy(out=m_picked[:], in_=xs[:].indirect(mix_sb[:]))
        place(q_scales, q_picked)
        w1_raw = shared.tile([P, PACK, H], F32, name="w1_raw", offset=20480, align_bytes=64)
        nc.sync.dma_start(out=w1_raw[:], in_=w1.rearrange("(p j) c -> p j c", j=PACK))
        nc.sync.dma_start(al_sb[:], al)
        w3_raw = shared.tile([P, PACK, N], F32, name="w3_raw", offset=8192, align_bytes=64)
        nc.sync.dma_start(out=w3_raw[:], in_=w3.rearrange("(p j) c -> p j c", j=PACK))
        place(m_scales, m_picked)
        nc.vector.tensor_copy(out=q_words[:], in_=xw[:].bitcast(U32).indirect(offs_sb[:]))
        m_words = [sb("m_words0", [P, CHUNK], U32)]
        nc.vector.tensor_copy(out=m_words[0][:], in_=xw[:].bitcast(U32).indirect(mix_sb[:, : CHUNK // LIST_ROWS]))

        def two_planes(raw, u):
            return by_four(raw)[:, :, :, 2 * u : 2 * u + 2]

        def dealt_pair(grouped):
            return grouped[:].rearrange("p (t m j) -> p m j t", t=2, j=PACK)

        def one_plane(grouped):
            return grouped[:].rearrange("p (m j) -> p m j", j=PACK)

        w2_low = [sb("w2_low%d" % t, [P, PACK * GROUPS], BF16) for t in range(2)]
        w2_high = shared.tile([P, PACK * P], BF16, name="w2_high", offset=29696, align_bytes=64)
        w2_pair = sb("w2_pair", [P, PACK * HALF], BF16)
        for t in range(2):
            nc.scalar.copy(out=one_plane(w2_low[t])[:, :, 0:2], in_=by_four(w2_left[0])[:, :, :, t])
        nc.scalar.copy(out=dealt_pair(w2_pair)[:, :GROUPS, 0:2], in_=two_planes(w2_left[0], 1))
        nc.scalar.copy(out=dealt_pair(w2_high)[:, :, 0:2], in_=two_planes(w2_left[1], 0))
        nc.scalar.copy(out=dealt_pair(w2_pair)[:, GROUPS:, 0:2], in_=two_planes(w2_left[1], 1))
        nc.vector.tensor_copy(out=dealt_pair(w2_high)[:, :, 2:4], in_=two_planes(w2_right, 0)[:, GROUPS:])
        for t in range(2):
            nc.scalar.copy(out=one_plane(w2_low[t])[:, :, 2:4], in_=by_four(w2_right)[:, :GROUPS, :, t])
        nc.scalar.copy(out=dealt_pair(w2_pair)[:, :, 2:4], in_=two_planes(w2_right, 1))
        w2_mx = [mx_tiles("w2_first", HALF)]
        for t, h in ((0, 0), (0, 1), (1, 1), (1, 0)):
            cols = slice(t * P + h * GROUPS, t * P + (h + 1) * GROUPS)
            grouped = w2_high[:, t * HALF : (t + 1) * HALF] if h else w2_low[t][:]
            nc.vector.quantize_mx(out=w2_mx[0][0][:, cols].bitcast(FP8X4), scales=w2_mx[0][1][:, cols], in_=grouped)
        m_words.append(shared.tile([P, S - CHUNK], U32, name="m_words1", offset=28672, align_bytes=64))
        nc.vector.tensor_copy(out=m_words[1][:], in_=xw[:].bitcast(U32).indirect(mix_sb[:, CHUNK // LIST_ROWS :]))
        late_codes = shared.tile([P, HALF], U32, name="w2_late_codes", offset=30208, align_bytes=64)
        w2_mx.append((late_codes, sb("w2_late_scales", [P, HALF], U8)))
        quantize(w2_mx[1], w2_pair, 0, HALF)
        w1_bf = shared.tile([P, PACK * H], BF16, name="w1_bf", offset=16384, align_bytes=64)
        halves = {}
        for t in range(PACK - 1):
            for h, tag in enumerate(("s%d" % t, "e%d" % (PACK - 1 - t))):
                bank = psum.tile([P, HALF], F32, name="s_half%d_%d" % (t, h), tag=tag)
                product(bank[:], w2_mx[t // 2], t % 2, (q_words, q_scales), slice(h * HALF, (h + 1) * HALF))
                halves[t, h] = bank
        s_last = psum.tile([P, S], F32, name="s_last", tag="s3")
        product(s_last[:], w2_mx[1], 1, (q_words, q_scales), slice(0, S))
        s_sb = [sb("s_sb%d" % t, [P, S], F32) for t in range(2)]
        s_sb.extend(shared.tile([P, S], F32, name="s_sb%d" % t, offset=16384 + 2048 * t, align_bytes=64) for t in (2, 3))
        mask_early = sb("mask_early", [P, PACK, 2 * CHUNK], F32)

        def look_up(mask, t, first, width):
            entries = al_sb[:, first // LIST_ROWS : (first + width) // LIST_ROWS]
            nc.scalar.activation(mask[:, t, :], s_sb[t][:].indirect(entries), ACT.Sigmoid)

        def empty(t, h, copy):
            copy(out=s_sb[t][:, h * HALF : (h + 1) * HALF], in_=halves[t, h][:])

        for t in range(2):
            for h in range(2):
                empty(t, h, nc.scalar.copy)
        for t in range(2):
            look_up(mask_early, t, 0, 2 * CHUNK)
        nc.vector.tensor_copy(out=dealt(w1_bf), in_=by_four(w1_raw))
        nc.vector.tensor_copy(out=s_sb[3][:], in_=s_last[:])
        for h in range(2):
            empty(2, h, nc.scalar.copy)
        for t in (3, 2):
            look_up(mask_early, t, 0, 2 * CHUNK)
        w1_mx = mx_tiles("w1", H)
        quantize(w1_mx, w1_bf, 0, H)
        e_banks = []
        for c in range(S // CHUNK):
            bank = psum.tile([P, PACK, CHUNK], F32, name="e_bank%d" % c, tag="e%d" % c)
            for t in range(PACK):
                words = m_words[0] if c == 0 else m_words[1][:, (c - 1) * CHUNK :]
                product(bank[:, t, :], w1_mx, t, (words, m_scales[:, c * CHUNK :]), slice(0, CHUNK))
            e_banks.append(bank)

        w3_mx = mx_tiles("w3", N - P)
        w3_last = (sb("w3_last_codes", [P, P], U32, on="mask_early"), sb("w3_last_scales", [P, P], U8))
        w3_cuts = (0, HALF, N - P, N)
        w3_bf = [
            shared.tile([P, PACK * (w3_cuts[i + 1] - w3_cuts[i])], BF16, name="w3_bf%d" % i, offset=(2048, 6144, 4032)[i], align_bytes=64)
            for i in range(3)
        ]

        def quantize_w3(i):
            nc.vector.quantize_mx(
                out=w3_mx[0][:, w3_cuts[i] : w3_cuts[i + 1]].bitcast(FP8X4),
                scales=w3_mx[1][:, w3_cuts[i] : w3_cuts[i + 1]],
                in_=w3_bf[i][:],
            )

        for i in range(2):
            nc.vector.tensor_copy(out=in_order(w3_bf[i]), in_=by_four(w3_raw)[:, w3_cuts[i] // PACK : w3_cuts[i + 1] // PACK])
        for i in range(2):
            quantize_w3(i)
        nc.gpsimd.tensor_scalar(
            out=w3_bf[2][:].rearrange("p (c j) -> p c j", j=PACK),
            in0=w3_raw[:, :, w3_cuts[2] :].rearrange("p j c -> p c j"),
            scalar1=1.0,
            scalar2=0.0,
            op0=ALU.mult,
            op1=ALU.add,
        )

        mask_late = [shared.tile([P, PACK, CHUNK], F32, name="mask%d" % c, offset=16384 + c * 2048, align_bytes=64) for c in range(2)]
        for c in range(2):
            for t in range(PACK):
                look_up(mask_late[c], t, (2 + c) * CHUNK, CHUNK)

        z_bf = shared.tile([P, PACK * 2 * CHUNK], BF16, name="z_bf", offset=1984, align_bytes=64)
        z_mx = [mx_tiles("z%d" % c, CHUNK) for c in range(S // CHUNK)]
        out_rows = out.rearrange("(m p) j -> p m j", p=P)

        def masked(c, dst):
            mask = mask_early if c < 2 else mask_late[c - 2]
            lo = c * CHUNK if c < 2 else 0
            nc.vector.scalar_tensor_tensor(
                out=dst.rearrange("p (n t) -> p n t", t=PACK),
                in0=e_banks[c][:].rearrange("p t n -> p n t"),
                scalar=0.0,
                in1=mask[:, :, lo : lo + CHUNK].rearrange("p t n -> p n t"),
                op0=ALU.max,
                op1=ALU.mult,
            )

        def z_of(c):
            return z_bf[:, c % 2 * PACK * CHUNK : (c % 2 + 1) * PACK * CHUNK]

        def decode(chunks, m0, count, tag):
            bank = psum.tile([P, count, len(chunks) * CHUNK], F32, name="o_bank%d_%d" % (chunks[0], m0), tag=tag)
            for i, c in enumerate(chunks):
                for m in range(count):
                    weights, block = (w3_last, 0) if m0 + m == PACK - 1 else (w3_mx, m0 + m)
                    product(bank[:, m, i * CHUNK : (i + 1) * CHUNK], weights, block, z_mx[c], slice(0, CHUNK))
            return bank

        def leave(c, m0, count, bank, copy, width=CHUNK):
            res = sb("res%d_%d" % (c, m0), [P, count, width], F32)
            copy(out=res[:], in_=bank[:])
            nc.sync.dma_start(out=out_rows[:, m0 : m0 + count, c * CHUNK : c * CHUNK + width], in_=res[:])

        masked(0, z_of(0))
        masked(1, z_of(1))
        quantize(z_mx[0], z_of(0), 0, CHUNK)
        quantize(z_mx[1], z_of(1), 0, CHUNK)
        quantize(w3_last, w3_bf[2], 0, P)
        bank0 = decode([0], 0, 2, "s0")
        bank1 = decode([1], 0, 2, "s3")
        bank01 = decode([0, 1], 2, 2, "s1")
        masked(2, z_of(2))
        leave(0, 0, 2, bank0, nc.vector.tensor_copy)
        quantize(z_mx[2], z_of(2), 0, CHUNK)
        bank2 = decode([2], 0, PACK, "s2")
        z_last = sb("z_last", [P, PACK * CHUNK], BF16, on="z0_codes")
        masked(3, z_last[:])
        quantize(z_mx[3], z_last, 0, CHUNK)
        leave(1, 0, 2, bank1, nc.scalar.copy)
        leave(0, 2, 2, bank01, nc.scalar.copy, 2 * CHUNK)
        leave(2, 0, PACK, bank2, nc.scalar.copy)
        leave(3, 0, 2, decode([3], 0, 2, "e1"), nc.scalar.copy)
        leave(3, 2, 2, decode([3], 2, 2, "e0"), nc.vector.tensor_copy)
